import numpy as np
import ml_dtypes


def mxq(x, axis, fmt="e4m3"):
    dtype, down = {"e4m3": (ml_dtypes.float8_e4m3fn, 7), "e5m2": (ml_dtypes.float8_e5m2, 14)}[fmt]
    v = np.moveaxis(np.asarray(x, np.float32).astype(ml_dtypes.bfloat16).astype(np.float64), axis, -1)
    blocks = v.reshape(v.shape[:-1] + (-1, 32))
    amax = np.abs(blocks).max(-1, keepdims=True)
    byte = np.maximum(np.where(amax > 0, np.frexp(amax)[1] - 1 + 127, 0) - down, 1)
    scale = np.exp2(byte - 127.0)
    codes = (blocks / scale).astype(np.float32).astype(dtype).astype(np.float64)
    return np.moveaxis((codes * scale).reshape(v.shape), -1, axis)


WIDE = False


def mx_kscale(k):
    if not WIDE:
        return np.ones(k)
    levels = np.array([10, -10, 5, -5, 0])
    if k % 512:
        return np.exp2(np.random.permutation(np.resize(levels, k // 32))).repeat(32)
    a = np.empty((k // 512, 16))
    for p in range(k // 512):
        a[p, :8] = np.random.permutation(np.resize(levels, 8))
        for g in range(8):
            far = levels[np.abs(levels - a[p, g]) >= 10]
            a[p, g + 8] = far[np.random.randint(len(far))]
    return np.exp2(a.ravel()).repeat(32)


def f64(x):
    return np.asarray(x).astype(np.float64)


def striped(idx):
    return np.tile(idx.reshape(-1, 16).T, (8, 1)).astype(np.uint16)


def unstriped(offs):
    return offs[:16].T.reshape(-1).astype(np.int64)


E2M1 = np.array([0.0, 0.5, 1.0, 1.5, 2.0, 3.0, 4.0, 6.0, -0.0, -0.5, -1.0, -1.5, -2.0, -3.0, -4.0, -6.0])


def pack_weight(w, fmt):
    k, n = w.shape
    w = f64(np.asarray(w, np.float32).astype(ml_dtypes.bfloat16)).reshape(k // 32, 32, n)
    amax = np.abs(w).max(1)
    if fmt == "e4m3":
        byte = np.frexp(amax)[1] - 1 + 127 - 7
    else:
        mant, ex = np.frexp(amax / 6.0)
        byte = np.where(mant > 0.5, ex, ex - 1) + 127
    byte = np.clip(np.where(amax > 0, byte, 1), 1, 254)
    scaled = (w * np.exp2(127.0 - byte)[:, None, :]).reshape(k, n).astype(np.float32)
    by_word = np.ascontiguousarray(scaled.reshape(k // 512, 128, 4, n).transpose(0, 1, 3, 2))
    if fmt == "e4m3":
        words = by_word.astype(ml_dtypes.float8_e4m3fn).view(np.uint8)
    else:
        c = by_word.astype(ml_dtypes.float4_e2m1fn).view(np.uint8) & 0xF
        words = (c[..., 0::2] | (c[..., 1::2] << 4)).reshape(k // 512, 128, 2 * n)
    return np.ascontiguousarray(words), np.ascontiguousarray(byte.astype(np.uint8).reshape(k // 512, 16, n))


def unpack_weight(words, scales, fmt):
    g, _, n = scales.shape
    words = np.ascontiguousarray(words).reshape(g, 128, n, -1)
    if fmt == "e4m3":
        vals = words.view(ml_dtypes.float8_e4m3fn).astype(np.float64)
    else:
        nib = np.empty((g, 128, n, 4), np.uint8)
        nib[..., 0::2] = words & 0xF
        nib[..., 1::2] = words >> 4
        vals = E2M1[nib]
    vals = vals * np.repeat(np.exp2(scales.astype(np.float64) - 127.0), 8, axis=1)[..., None]
    return vals.transpose(0, 1, 3, 2).reshape(g * 512, n)


def gelu(v):
    return 0.5 * v * (1.0 + np.tanh(np.sqrt(2.0 / np.pi) * (v + 0.044715 * v**3)))


K, R, N, T, S, T2 = 1024, 512, 1024, 2048, 1024, 2048

def setup_inputs():
    n = np.random.standard_normal
    s = mx_kscale(K)[:, None]
    u = mx_kscale(R)[:, None]
    tab_words, tab_scales = pack_weight(n((K, T)) * s, "e4m3")
    wx_words, wx_scales = pack_weight(n((K, N)) / np.sqrt(K) / s, "e4m3")
    wu_words, wu_scales = pack_weight(n((R, N)) / np.sqrt(R) / u, "e2m1")
    return {
        "tab_words": tab_words, "tab_scales": tab_scales,
        "offs": striped(np.random.permutation(T)[:S]),
        "w1": (n((K, R)) / np.sqrt(K) / s * u.T).astype(np.float32),
        "wx_words": wx_words, "wx_scales": wx_scales,
        "wu_words": wu_words, "wu_scales": wu_scales,
        "b2": (0.5 * n(N)).astype(np.float32),
        "wgo": np.exp(0.3 * n((128, S))).astype(np.float32),
        "offs2": striped(np.random.permutation(T2)[:S]),
    }

def reference(tab_words, tab_scales, offs, w1, wx_words, wx_scales, wu_words, wu_scales, b2, wgo, offs2):
    v = unpack_weight(tab_words, tab_scales, "e4m3")[:, unstriped(offs)]
    wx = unpack_weight(wx_words, wx_scales, "e4m3")
    wu = unpack_weight(wu_words, wu_scales, "e2m1")
    x = wx.T @ v
    h = np.maximum(mxq(f64(w1), 0, "e4m3").T @ v, 0.0)
    c = (wu.T @ mxq(h, 0, "e4m3")) + f64(b2)[:, None]
    y = x * c + x
    out = np.zeros((N, T2))
    out[:, unstriped(offs2)] = np.tile(f64(wgo), (N // 128, 1)) * y
    return out

@@ -1,0 +1,225 @@
+from contextlib import ExitStack
+
+import concourse.mybir as mybir
+
+K, R, N, T, S, T2 = 1024, 512, 1024, 2048, 1024, 2048
+FLOPS = 2 * S * (K * N + K * R + R * N)
+
+F32 = mybir.dt.float32
+BF16 = mybir.dt.bfloat16
+I32 = mybir.dt.int32
+U32 = mybir.dt.uint32
+U16 = mybir.dt.uint16
+U8 = mybir.dt.uint8
+FP8X4 = mybir.dt.float8_e4m3fn_x4
+FP4X4 = mybir.dt.float4_e2m1fn_x4
+MULT = mybir.AluOpType.mult
+ADD = mybir.AluOpType.add
+ACT = mybir.ActivationFunctionType
+
+P = 128
+PASSES = K // 512
+CHUNK = 256
+CHUNKS = S // CHUNK
+GROUP = 128
+BANK = 512
+TILES = N // P
+EARLY = 256
+MODE = "B"
+
+
+def tile_list_auction_lowrank_cross_kernel(
+    tc, tab_words, tab_scales, offs, w1, wx_words, wx_scales, wu_words, wu_scales, b2, wgo, offs2, out
+):
+    nc = tc.nc
+    with ExitStack() as ctx:
+        keep = ctx.enter_context(tc.tile_pool(name="keep", bufs=1))
+        ring = ctx.enter_context(tc.tile_pool(name="ring", bufs=2))
+        ps_h = ctx.enter_context(tc.psum_pool(name="ps_h", bufs=2))
+        ps_x = ctx.enter_context(tc.psum_pool(name="ps_x", bufs=3))
+        ps_c = ctx.enter_context(tc.psum_pool(name="ps_c", bufs=3))
+
+        gather_offs = keep.tile([P, S // 16], U16, name="gather_offs")
+        scatter_offs = keep.tile([P, S // 16], U16, name="scatter_offs")
+        tab_w = [keep.tile([P, T], I32, name=f"tab_w{a}", align_bytes=64) for a in range(PASSES)]
+        tab_s = keep.tile([P, T], U8, name="tab_s", align_bytes=64)
+        v_w = [keep.tile([P, S], U32, name=f"v_w{a}", align_bytes=64) for a in range(PASSES)]
+        v_s = keep.tile([P, S], U8, name="v_s", align_bytes=64)
+        w1_raw = [keep.tile([P, 4, R], F32, name=f"w1_raw{a}", align_bytes=64) for a in range(PASSES)]
+        w1_bf = [keep.tile([P, 4 * R], BF16, name=f"w1_bf{a}", align_bytes=64) for a in range(PASSES)]
+        w1_w = [keep.tile([P, R], U32, name=f"w1_w{a}", align_bytes=64) for a in range(PASSES)]
+        w1_s = [keep.tile([P, R], U8, name=f"w1_s{a}", align_bytes=64) for a in range(PASSES)]
+        wx_w = keep.tile([P, PASSES, N], I32, name="wx_w", align_bytes=64)
+        wx_s = keep.tile([P, N], U8, name="wx_s", align_bytes=64)
+        wu_w = keep.tile([P, 2 * N], U8, name="wu_w", align_bytes=64)
+        wu_s = keep.tile([P, N], U8, name="wu_s", align_bytes=64)
+        h_bf = keep.tile([P, 4 * S], BF16, name="h_bf", align_bytes=64)
+        h_w = keep.tile([P, S], U32, name="h_w", align_bytes=64)
+        h_s = keep.tile([P, S], U8, name="h_s", align_bytes=64)
+        wgo_sb = keep.tile([P, S], F32, name="wgo_sb", align_bytes=64)
+        b2_sb = keep.tile([P, TILES], F32, name="b2_sb")
+        bias = keep.tile([P, TILES], F32, name="bias")
+        cache = [keep.tile([P, T2], F32, name=f"cache{b}", align_bytes=64) for b in range(2)]
+
+        for plane in (tab_s, wx_s, wu_s):
+            nc.vector.memset(plane[:].bitcast(I32), 0)
+
+        def load_w1(a):
+            nc.sync.dma_start(w1_raw[a][:], w1[512 * a : 512 * (a + 1), :].rearrange("(p j) r -> p j r", j=4))
+
+        def load_table(a):
+            nc.sync.dma_start(tab_w[a][:], tab_words[a].rearrange("p t i -> p (t i)").bitcast(I32))
+
+        def load_scales(queue, plane, src, passes):
+            for q in range(4):
+                queue.dma_start(
+                    plane[32 * q : 32 * q + 4 * passes, :].bitcast(I32), src[:, 4 * q : 4 * q + 4, :].bitcast(I32)
+                )
+
+        wx_src = wx_words.rearrange("a p e i -> p a (e i)").bitcast(I32)
+        nc.sync.dma_start(gather_offs[:], offs)
+        load_w1(0)
+        load_w1(1)
+        load_scales(nc.sync, tab_s, tab_scales, PASSES)
+        load_table(0)
+        load_table(1)
+        load_scales(nc.sync, wx_s, wx_scales, PASSES)
+        nc.sync.dma_start(wx_w[:, :, 0:EARLY], wx_src[:, :, 0:EARLY])
+        nc.sync.dma_start(wgo_sb[:], wgo)
+        load_scales(nc.sync, wu_s, wu_scales, 1)
+        nc.sync.dma_start(wu_w[:].bitcast(I32), wu_words[0].bitcast(I32))
+        with nc.allow_non_contiguous_dma(reason="one bias value to a partition"):
+            nc.sync.dma_start(b2_sb[:], b2.rearrange("(i p) -> p i", p=P))
+        nc.sync.dma_start(scatter_offs[:], offs2)
+        nc.sync.dma_start(wx_w[:, :, EARLY:N], wx_src[:, :, EARLY:N])
+
+        for tile in cache:
+            nc.vector.memset(tile[:, 0:1024], 0.0)
+            nc.vector.memset(tile[:, 1024:T2], 0.0)
+
+        for a in range(PASSES):
+            dst = w1_bf[a][:].rearrange("p (t m j) -> p m t j", t=4, j=4)
+            src = w1_raw[a][:].rearrange("p j (m t) -> p m t j", t=4)
+            nc.vector.tensor_copy(dst[:, 0:64], src[:, 0:64])
+            nc.scalar.copy(dst[:, 64:128], src[:, 64:128])
+            nc.vector.quantize_mx(out=w1_w[a][:].bitcast(FP8X4), scales=w1_s[a][:], in_=w1_bf[a][:])
+
+        nc.gpsimd.tensor_scalar(bias[:], b2_sb[:], 1.0, None, ADD)
+
+        def gather_scales(q):
+            lst = gather_offs[:, q * CHUNK // 16 : (q + 1) * CHUNK // 16]
+            nc.vector.tensor_copy(v_s[:, q * CHUNK : (q + 1) * CHUNK], tab_s[:].indirect(lst))
+
+        def gather_words(a, q):
+            lst = gather_offs[:, q * CHUNK // 16 : (q + 1) * CHUNK // 16]
+            nc.vector.tensor_copy(v_w[a][:, q * CHUNK : (q + 1) * CHUNK], tab_w[a][:].bitcast(U32).indirect(lst))
+
+        def rank_space(q):
+            for g in range(q * CHUNK // GROUP, (q + 1) * CHUNK // GROUP):
+                cols = slice(g * GROUP, (g + 1) * GROUP)
+                acc = ps_h.tile([P, 4, GROUP], F32, name="acc_h")
+                for t in range(4):
+                    for a in range(PASSES):
+                        nc.tensor.matmul_mx(
+                            out=acc[:, t, :],
+                            lhsT=w1_w[a][:, t * P : (t + 1) * P].bitcast(FP8X4),
+                            lhsT_scale=w1_s[a][:, t * P : (t + 1) * P],
+                            rhs=v_w[a][:, cols].bitcast(FP8X4),
+                            rhs_scale=v_s[4 * a : P, cols],
+                            start=(a == 0),
+                            stop=(a == PASSES - 1),
+                        )
+                nc.scalar.activation(
+                    h_bf[:, 4 * g * GROUP : 4 * (g + 1) * GROUP].rearrange("p (n t) -> p n t", t=4),
+                    acc[:].rearrange("p t n -> p n t"),
+                    ACT.Relu,
+                )
+            cols = slice(q * CHUNK, (q + 1) * CHUNK)
+            nc.vector.quantize_mx(
+                out=h_w[:, cols].bitcast(FP8X4), scales=h_s[:, cols], in_=h_bf[:, 4 * q * CHUNK : 4 * (q + 1) * CHUNK]
+            )
+
+        def project(i, lo, hi):
+            acc = ps_x.tile([P, hi - lo], F32, name="acc_x")
+            for a in range(PASSES):
+                nc.tensor.matmul_mx(
+                    out=acc[:],
+                    lhsT=wx_w[:, a, i * P : (i + 1) * P].bitcast(FP8X4),
+                    lhsT_scale=wx_s[4 * a : P, i * P : (i + 1) * P],
+                    rhs=v_w[a][:, lo:hi].bitcast(FP8X4),
+                    rhs_scale=v_s[4 * a : P, lo:hi],
+                    start=(a == 0),
+                    stop=(a == PASSES - 1),
+                )
+            return acc
+
+        def cross(i, lo, hi):
+            acc = ps_c.tile([P, hi - lo], F32, name="acc_c")
+            nc.tensor.matmul_mx(
+                out=acc[:],
+                lhsT=wu_w[:, 2 * i * P : 2 * (i + 1) * P].bitcast(FP4X4),
+                lhsT_scale=wu_s[:, i * P : (i + 1) * P],
+                rhs=h_w[:, lo:hi].bitcast(FP8X4),
+                rhs_scale=h_s[:, lo:hi],
+                start=True,
+                stop=True,
+            )
+            return acc
+
+        def features(i, lo, hi, on_vector):
+            width = hi - lo
+            step = min(width, BANK)
+            x_sb = ring.tile([P, width], F32, name="x_sb", align_bytes=64)
+            y_sb = ring.tile([P, width], F32, name="y_sb", align_bytes=64, bufs=3)
+            for c in range(0, width, step):
+                acc = project(i, lo + c, lo + c + step)
+                nc.scalar.copy(x_sb[:, c : c + step], acc[:])
+            if MODE == "A":
+                xw_sb = x_sb
+            else:
+                xw_sb = ring.tile([P, width], F32, name="xw_sb", align_bytes=64)
+                if MODE == "B":
+                    nc.gpsimd.tensor_tensor(xw_sb[:], x_sb[:], wgo_sb[:, lo:hi], MULT)
+                else:
+                    nc.vector.tensor_tensor(xw_sb[:], x_sb[:], wgo_sb[:, lo:hi], MULT)
+            if on_vector:
+                for c in range(0, width, step):
+                    acc = cross(i, lo + c, lo + c + step)
+                    nc.vector.scalar_tensor_tensor(
+                        y_sb[:, c : c + step], acc[:], bias[:, i : i + 1], xw_sb[:, c : c + step], ADD, MULT
+                    )
+            else:
+                c_sb = ring.tile([P, width], F32, name="c_sb", align_bytes=64)
+                for c in range(0, width, step):
+                    acc = cross(i, lo + c, lo + c + step)
+                    nc.scalar.activation(c_sb[:, c : c + step], acc[:], ACT.Identity, bias=bias[:, i : i + 1])
+                nc.gpsimd.tensor_tensor(y_sb[:], xw_sb[:], c_sb[:], MULT)
+            return y_sb
+
+        def scatter(i, lo, hi, y_sb):
+            window = cache[i % 2][:].indirect(scatter_offs[:, lo // 16 : hi // 16])
+            if MODE == "A":
+                nc.vector.tensor_tensor(window, y_sb[:], wgo_sb[:, lo:hi], MULT)
+            else:
+                nc.vector.tensor_copy(window, y_sb[:])
+
+        for q in range(2):
+            gather_scales(q)
+            gather_words(0, q)
+        gather_words(1, 0)
+        rank_space(0)
+        first = features(0, 0, CHUNK, True)
+        gather_words(1, 1)
+        rank_space(1)
+        for q in range(2, CHUNKS):
+            gather_scales(q)
+            gather_words(0, q)
+            gather_words(1, q)
+            rank_space(q)
+        scatter(0, 0, CHUNK, first)
+        for q in range(1, CHUNKS):
+            scatter(0, q * CHUNK, (q + 1) * CHUNK, features(0, q * CHUNK, (q + 1) * CHUNK, True))
+        nc.sync.dma_start(out[0:P, :], cache[0][:])
+        for i in range(1, TILES):
+            scatter(i, 0, S, features(i, 0, S, MODE != "B"))
+            nc.sync.dma_start(out[i * P : (i + 1) * P, :], cache[i % 2][:])

@@ -1,6 +1,7 @@
 from contextlib import ExitStack
 
 import concourse.mybir as mybir
+from concourse.masks import make_identity
 
 K, R, N, T, S, T2 = 1024, 512, 1024, 2048, 1024, 2048
 FLOPS = 2 * S * (K * N + K * R + R * N)
@@ -18,14 +19,14 @@ ADD = mybir.AluOpType.add
 ACT = mybir.ActivationFunctionType
 
 P = 128
-PASSES = K // 512
-CHUNK = 256
-CHUNKS = S // CHUNK
-GROUP = 128
-BANK = 512
+PACK = 4
+PASSES = K // (P * PACK)
 TILES = N // P
-EARLY = 256
-MODE = "B"
+HALF = 512
+QUARTER = 256
+GROUP = 128
+CAST_SPLIT = 64
+H_BANKS = (0, 1, 0, 1, 4, 0, 1, 0)
 
 
 def tile_list_auction_lowrank_cross_kernel(
@@ -35,40 +36,32 @@ def tile_list_auction_lowrank_cross_kernel(
     with ExitStack() as ctx:
         keep = ctx.enter_context(tc.tile_pool(name="keep", bufs=1))
         ring = ctx.enter_context(tc.tile_pool(name="ring", bufs=2))
-        ps_h = ctx.enter_context(tc.psum_pool(name="ps_h", bufs=2))
-        ps_x = ctx.enter_context(tc.psum_pool(name="ps_x", bufs=3))
-        ps_c = ctx.enter_context(tc.psum_pool(name="ps_c", bufs=3))
+        psum = ctx.enter_context(tc.psum_pool(name="psum", bufs=1))
+
+        def bank(b, shape):
+            return psum.tile(shape, F32, name=f"bank{b}")
 
         gather_offs = keep.tile([P, S // 16], U16, name="gather_offs")
         scatter_offs = keep.tile([P, S // 16], U16, name="scatter_offs")
-        tab_w = [keep.tile([P, T], I32, name=f"tab_w{a}", align_bytes=64) for a in range(PASSES)]
         tab_s = keep.tile([P, T], U8, name="tab_s", align_bytes=64)
         v_w = [keep.tile([P, S], U32, name=f"v_w{a}", align_bytes=64) for a in range(PASSES)]
-        v_s = keep.tile([P, S], U8, name="v_s", align_bytes=64)
-        w1_raw = [keep.tile([P, 4, R], F32, name=f"w1_raw{a}", align_bytes=64) for a in range(PASSES)]
-        w1_bf = [keep.tile([P, 4 * R], BF16, name=f"w1_bf{a}", align_bytes=64) for a in range(PASSES)]
+        v_s = [keep.tile([P, HALF], U8, name="v_s", align_bytes=64)]
+        w1_raw = [keep.tile([P, PACK, R], F32, name=f"w1_raw{a}", align_bytes=64) for a in range(PASSES)]
+        w1_bf = [keep.tile([P, PACK * R], BF16, name=f"w1_bf{a}", align_bytes=64) for a in range(PASSES)]
         w1_w = [keep.tile([P, R], U32, name=f"w1_w{a}", align_bytes=64) for a in range(PASSES)]
         w1_s = [keep.tile([P, R], U8, name=f"w1_s{a}", align_bytes=64) for a in range(PASSES)]
-        wx_w = keep.tile([P, PASSES, N], I32, name="wx_w", align_bytes=64)
         wx_s = keep.tile([P, N], U8, name="wx_s", align_bytes=64)
-        wu_w = keep.tile([P, 2 * N], U8, name="wu_w", align_bytes=64)
         wu_s = keep.tile([P, N], U8, name="wu_s", align_bytes=64)
-        h_bf = keep.tile([P, 4 * S], BF16, name="h_bf", align_bytes=64)
+        h_bf = keep.tile([P, PACK * S], BF16, name="h_bf", align_bytes=64)
         h_w = keep.tile([P, S], U32, name="h_w", align_bytes=64)
         h_s = keep.tile([P, S], U8, name="h_s", align_bytes=64)
-        wgo_sb = keep.tile([P, S], F32, name="wgo_sb", align_bytes=64)
-        b2_sb = keep.tile([P, TILES], F32, name="b2_sb")
+        b2_rows = keep.tile([P, P], F32, name="b2_rows", align_bytes=64)
+        ident = keep.tile([P, P], F32, name="ident", align_bytes=64)
         bias = keep.tile([P, TILES], F32, name="bias")
         cache = [keep.tile([P, T2], F32, name=f"cache{b}", align_bytes=64) for b in range(2)]
 
         for plane in (tab_s, wx_s, wu_s):
             nc.vector.memset(plane[:].bitcast(I32), 0)
-
-        def load_w1(a):
-            nc.sync.dma_start(w1_raw[a][:], w1[512 * a : 512 * (a + 1), :].rearrange("(p j) r -> p j r", j=4))
-
-        def load_table(a):
-            nc.sync.dma_start(tab_w[a][:], tab_words[a].rearrange("p t i -> p (t i)").bitcast(I32))
 
         def load_scales(queue, plane, src, passes):
             for q in range(4):
@@ -76,85 +69,98 @@ def tile_list_auction_lowrank_cross_kernel(
                     plane[32 * q : 32 * q + 4 * passes, :].bitcast(I32), src[:, 4 * q : 4 * q + 4, :].bitcast(I32)
                 )
 
-        wx_src = wx_words.rearrange("a p e i -> p a (e i)").bitcast(I32)
+        nc.sync.dma_start(
+            b2_rows[:], b2.rearrange("(i p) -> i p", p=P).unsqueeze(0).broadcast_to([P // TILES, TILES, P])
+        )
         nc.sync.dma_start(gather_offs[:], offs)
-        load_w1(0)
-        load_w1(1)
-        load_scales(nc.sync, tab_s, tab_scales, PASSES)
-        load_table(0)
-        load_table(1)
-        load_scales(nc.sync, wx_s, wx_scales, PASSES)
-        nc.sync.dma_start(wx_w[:, :, 0:EARLY], wx_src[:, :, 0:EARLY])
-        nc.sync.dma_start(wgo_sb[:], wgo)
-        load_scales(nc.sync, wu_s, wu_scales, 1)
-        nc.sync.dma_start(wu_w[:].bitcast(I32), wu_words[0].bitcast(I32))
-        with nc.allow_non_contiguous_dma(reason="one bias value to a partition"):
-            nc.sync.dma_start(b2_sb[:], b2.rearrange("(i p) -> p i", p=P))
+        for a in range(PASSES):
+            rows = w1[P * PACK * a : P * PACK * (a + 1), :]
+            nc.sync.dma_start(w1_raw[a][:], rows.rearrange("(p j) r -> p j r", j=PACK))
         nc.sync.dma_start(scatter_offs[:], offs2)
-        nc.sync.dma_start(wx_w[:, :, EARLY:N], wx_src[:, :, EARLY:N])
+        load_scales(nc.sync, tab_s, tab_scales, PASSES)
+
+        make_identity(nc, ident[:])
+        b2_cols = bank(7, [P, P])
+        nc.tensor.transpose(b2_cols[:], b2_rows[:], ident[:])
+        nc.scalar.activation(bias[:], b2_cols[:, 0:TILES], ACT.Copy, bias=1.0)
+
+        tab_w = [keep.tile([P, T], I32, name=name, align_bytes=64) for name in ("ident", "b2_rows")]
+        for a in range(PASSES):
+            nc.sync.dma_start(tab_w[a][:], tab_words[a].rearrange("p t i -> p (t i)").bitcast(I32))
+        load_scales(nc.gpsimd, wx_s, wx_scales, PASSES)
+        load_scales(nc.gpsimd, wu_s, wu_scales, 1)
 
         for tile in cache:
-            nc.vector.memset(tile[:, 0:1024], 0.0)
-            nc.vector.memset(tile[:, 1024:T2], 0.0)
+            nc.vector.memset(tile[:, 0 : T2 // 2], 0.0)
+            nc.vector.memset(tile[:, T2 // 2 : T2], 0.0)
 
         for a in range(PASSES):
-            dst = w1_bf[a][:].rearrange("p (t m j) -> p m t j", t=4, j=4)
-            src = w1_raw[a][:].rearrange("p j (m t) -> p m t j", t=4)
-            nc.vector.tensor_copy(dst[:, 0:64], src[:, 0:64])
-            nc.scalar.copy(dst[:, 64:128], src[:, 64:128])
+            dst = w1_bf[a][:].rearrange("p (t m j) -> p m t j", t=PACK, j=PACK)
+            src = w1_raw[a][:].rearrange("p j (m t) -> p m t j", t=PACK)
+            nc.vector.tensor_copy(dst[:, 0:CAST_SPLIT], src[:, 0:CAST_SPLIT])
+            nc.scalar.copy(dst[:, CAST_SPLIT:P], src[:, CAST_SPLIT:P])
             nc.vector.quantize_mx(out=w1_w[a][:].bitcast(FP8X4), scales=w1_s[a][:], in_=w1_bf[a][:])
 
-        nc.gpsimd.tensor_scalar(bias[:], b2_sb[:], 1.0, None, ADD)
+        wx_src = wx_words.rearrange("a p e i -> p a (e i)").bitcast(I32)
+        wx_first = keep.tile([P, PASSES, P], I32, name="w1_raw0", align_bytes=64)
+        nc.sync.dma_start(wx_first[:], wx_src[:, :, 0:P])
+        wgo_sb = keep.tile([P, S], F32, name="w1_bf0", align_bytes=64)
+        nc.sync.dma_start(wgo_sb[:], wgo)
+        wu_w = keep.tile([P, 2 * N], U8, name="w1_raw1", align_bytes=64)
+        nc.sync.dma_start(wu_w[:].bitcast(I32), wu_words[0].bitcast(I32))
+        wx_rest = keep.tile([P, PASSES, N - P], I32, name="w1_bf1", align_bytes=64)
+        nc.sync.dma_start(wx_rest[:], wx_src[:, :, P:N])
 
-        def gather_scales(q):
-            lst = gather_offs[:, q * CHUNK // 16 : (q + 1) * CHUNK // 16]
-            nc.vector.tensor_copy(v_s[:, q * CHUNK : (q + 1) * CHUNK], tab_s[:].indirect(lst))
+        def v_plane(a, lo, hi):
+            return v_s[lo // HALF][4 * a : P, lo % HALF : lo % HALF + hi - lo]
 
-        def gather_words(a, q):
-            lst = gather_offs[:, q * CHUNK // 16 : (q + 1) * CHUNK // 16]
-            nc.vector.tensor_copy(v_w[a][:, q * CHUNK : (q + 1) * CHUNK], tab_w[a][:].bitcast(U32).indirect(lst))
+        def gather_scales(lo, hi):
+            nc.vector.tensor_copy(v_plane(0, lo, hi), tab_s[:].indirect(gather_offs[:, lo // 16 : hi // 16]))
 
-        def rank_space(q):
-            for g in range(q * CHUNK // GROUP, (q + 1) * CHUNK // GROUP):
-                cols = slice(g * GROUP, (g + 1) * GROUP)
-                acc = ps_h.tile([P, 4, GROUP], F32, name="acc_h")
-                for t in range(4):
+        def gather_words(a, lo, hi):
+            window = tab_w[a][:].bitcast(U32).indirect(gather_offs[:, lo // 16 : hi // 16])
+            nc.vector.tensor_copy(v_w[a][:, lo:hi], window)
+
+        def rank_space(lo, hi):
+            for g in range(lo // GROUP, hi // GROUP):
+                acc = bank(H_BANKS[g], [P, PACK, GROUP])
+                for t in range(PACK):
                     for a in range(PASSES):
                         nc.tensor.matmul_mx(
                             out=acc[:, t, :],
                             lhsT=w1_w[a][:, t * P : (t + 1) * P].bitcast(FP8X4),
                             lhsT_scale=w1_s[a][:, t * P : (t + 1) * P],
-                            rhs=v_w[a][:, cols].bitcast(FP8X4),
-                            rhs_scale=v_s[4 * a : P, cols],
+                            rhs=v_w[a][:, g * GROUP : (g + 1) * GROUP].bitcast(FP8X4),
+                            rhs_scale=v_plane(a, g * GROUP, (g + 1) * GROUP),
                             start=(a == 0),
                             stop=(a == PASSES - 1),
                         )
                 nc.scalar.activation(
-                    h_bf[:, 4 * g * GROUP : 4 * (g + 1) * GROUP].rearrange("p (n t) -> p n t", t=4),
-                    acc[:].rearrange("p t n -> p n t"),
+                    h_bf[:, PACK * g * GROUP : PACK * (g + 1) * GROUP].rearrange("p (j t) -> p j t", t=PACK),
+                    acc[:].rearrange("p t j -> p j t"),
                     ACT.Relu,
                 )
-            cols = slice(q * CHUNK, (q + 1) * CHUNK)
             nc.vector.quantize_mx(
-                out=h_w[:, cols].bitcast(FP8X4), scales=h_s[:, cols], in_=h_bf[:, 4 * q * CHUNK : 4 * (q + 1) * CHUNK]
+                out=h_w[:, lo:hi].bitcast(FP8X4), scales=h_s[:, lo:hi], in_=h_bf[:, PACK * lo : PACK * hi]
             )
 
-        def project(i, lo, hi):
-            acc = ps_x.tile([P, hi - lo], F32, name="acc_x")
+        def weighted_x(i, lo, hi, b, x_sb, xw_sb):
+            acc = bank(b, [P, hi - lo])
             for a in range(PASSES):
                 nc.tensor.matmul_mx(
                     out=acc[:],
-                    lhsT=wx_w[:, a, i * P : (i + 1) * P].bitcast(FP8X4),
+                    lhsT=(wx_first[:, a, :] if i == 0 else wx_rest[:, a, (i - 1) * P : i * P]).bitcast(FP8X4),
                     lhsT_scale=wx_s[4 * a : P, i * P : (i + 1) * P],
                     rhs=v_w[a][:, lo:hi].bitcast(FP8X4),
-                    rhs_scale=v_s[4 * a : P, lo:hi],
+                    rhs_scale=v_plane(a, lo, hi),
                     start=(a == 0),
                     stop=(a == PASSES - 1),
                 )
-            return acc
+            nc.scalar.copy(x_sb[:], acc[:])
+            nc.gpsimd.tensor_tensor(xw_sb[:, lo:hi], x_sb[:], wgo_sb[:, lo:hi], MULT)
 
-        def cross(i, lo, hi):
-            acc = ps_c.tile([P, hi - lo], F32, name="acc_c")
+        def cross(i, lo, hi, b):
+            acc = bank(b, [P, hi - lo])
             nc.tensor.matmul_mx(
                 out=acc[:],
                 lhsT=wu_w[:, 2 * i * P : 2 * (i + 1) * P].bitcast(FP4X4),
@@ -166,60 +172,55 @@ def tile_list_auction_lowrank_cross_kernel(
             )
             return acc
 
-        def features(i, lo, hi, on_vector):
-            width = hi - lo
-            step = min(width, BANK)
-            x_sb = ring.tile([P, width], F32, name="x_sb", align_bytes=64)
-            y_sb = ring.tile([P, width], F32, name="y_sb", align_bytes=64, bufs=3)
-            for c in range(0, width, step):
-                acc = project(i, lo + c, lo + c + step)
-                nc.scalar.copy(x_sb[:, c : c + step], acc[:])
-            if MODE == "A":
-                xw_sb = x_sb
-            else:
-                xw_sb = ring.tile([P, width], F32, name="xw_sb", align_bytes=64)
-                if MODE == "B":
-                    nc.gpsimd.tensor_tensor(xw_sb[:], x_sb[:], wgo_sb[:, lo:hi], MULT)
-                else:
-                    nc.vector.tensor_tensor(xw_sb[:], x_sb[:], wgo_sb[:, lo:hi], MULT)
-            if on_vector:
-                for c in range(0, width, step):
-                    acc = cross(i, lo + c, lo + c + step)
-                    nc.vector.scalar_tensor_tensor(
-                        y_sb[:, c : c + step], acc[:], bias[:, i : i + 1], xw_sb[:, c : c + step], ADD, MULT
-                    )
-            else:
-                c_sb = ring.tile([P, width], F32, name="c_sb", align_bytes=64)
-                for c in range(0, width, step):
-                    acc = cross(i, lo + c, lo + c + step)
-                    nc.scalar.activation(c_sb[:, c : c + step], acc[:], ACT.Identity, bias=bias[:, i : i + 1])
-                nc.gpsimd.tensor_tensor(y_sb[:], xw_sb[:], c_sb[:], MULT)
-            return y_sb
+        def finish_on_vector(i, lo, hi, b, xw_sb, y_sb):
+            acc = cross(i, lo, hi, b)
+            nc.vector.scalar_tensor_tensor(y_sb[:, lo:hi], acc[:], bias[:, i : i + 1], xw_sb[:, lo:hi], ADD, MULT)
+
+        def finish_on_gpsimd(i, lo, hi, b, xw_sb, y_sb):
+            c_sb = ring.tile([P, hi - lo], F32, name="c_sb", align_bytes=64, bufs=3)
+            acc = cross(i, lo, hi, b)
+            nc.scalar.activation(c_sb[:], acc[:], ACT.Identity, bias=bias[:, i : i + 1])
+            nc.gpsimd.tensor_tensor(y_sb[:, lo:hi], xw_sb[:, lo:hi], c_sb[:], MULT)
+
+        def x_tile(width):
+            return ring.tile([P, width], F32, name="x_sb", align_bytes=64, bufs=3)
 
         def scatter(i, lo, hi, y_sb):
             window = cache[i % 2][:].indirect(scatter_offs[:, lo // 16 : hi // 16])
-            if MODE == "A":
-                nc.vector.tensor_tensor(window, y_sb[:], wgo_sb[:, lo:hi], MULT)
-            else:
-                nc.vector.tensor_copy(window, y_sb[:])
+            nc.vector.tensor_copy(window, y_sb[:, lo:hi])
 
-        for q in range(2):
-            gather_scales(q)
-            gather_words(0, q)
-        gather_words(1, 0)
-        rank_space(0)
-        first = features(0, 0, CHUNK, True)
-        gather_words(1, 1)
-        rank_space(1)
-        for q in range(2, CHUNKS):
-            gather_scales(q)
-            gather_words(0, q)
-            gather_words(1, q)
-            rank_space(q)
-        scatter(0, 0, CHUNK, first)
-        for q in range(1, CHUNKS):
-            scatter(0, q * CHUNK, (q + 1) * CHUNK, features(0, q * CHUNK, (q + 1) * CHUNK, True))
+        xw_sb = ring.tile([P, S], F32, name="xw_sb", align_bytes=64)
+        y_sb = ring.tile([P, S], F32, name="y_sb", align_bytes=64, bufs=3)
+        gather_scales(0, HALF)
+        gather_words(0, 0, HALF)
+        gather_words(1, 0, QUARTER)
+        weighted_x(0, 0, QUARTER, 2, keep.tile([P, QUARTER], F32, name="x_first", align_bytes=64), xw_sb)
+        v_s.append(keep.tile([P, HALF], U8, name="x_first", align_bytes=64))
+        rank_space(0, QUARTER)
+        finish_on_vector(0, 0, QUARTER, 4, xw_sb, y_sb)
+        gather_words(1, QUARTER, HALF)
+        rank_space(QUARTER, HALF)
+        weighted_x(0, QUARTER, HALF, 3, x_tile(QUARTER), xw_sb)
+        finish_on_vector(0, QUARTER, HALF, 5, xw_sb, y_sb)
+        gather_scales(HALF, S)
+        for a in range(PASSES):
+            gather_words(a, HALF, S)
+        rank_space(HALF, S)
+        weighted_x(0, HALF, S, 2, x_tile(HALF), xw_sb)
+        finish_on_vector(0, HALF, S, 6, xw_sb, y_sb)
+        for lo, hi in ((0, QUARTER), (QUARTER, HALF), (HALF, S)):
+            scatter(0, lo, hi, y_sb)
         nc.sync.dma_start(out[0:P, :], cache[0][:])
+
         for i in range(1, TILES):
-            scatter(i, 0, S, features(i, 0, S, MODE != "B"))
+            xw_sb = ring.tile([P, S], F32, name="xw_sb", align_bytes=64)
+            y_sb = ring.tile([P, S], F32, name="y_sb", align_bytes=64, bufs=3)
+            x_banks, c_banks = ((2, 3), (0, 1)) if i % 2 else ((4, 5), (6, 7))
+            for c in range(2):
+                weighted_x(i, c * HALF, (c + 1) * HALF, x_banks[c], x_tile(HALF), xw_sb)
+                finish_on_gpsimd(i, c * HALF, (c + 1) * HALF, c_banks[c], xw_sb, y_sb)
+                if i == 1:
+                    scatter(i, c * HALF, (c + 1) * HALF, y_sb)
+            if i > 1:
+                scatter(i, 0, S, y_sb)
             nc.sync.dma_start(out[i * P : (i + 1) * P, :], cache[i % 2][:])

@@ -25,8 +25,9 @@ TILES = N // P
 HALF = 512
 QUARTER = 256
 GROUP = 128
-CAST_SPLIT = 64
-H_BANKS = (0, 1, 0, 1, 4, 0, 1, 0)
+CAST_SPLIT = 32
+WX_ROW = 4
+FIRST_TILES = 2
 
 
 def tile_list_auction_lowrank_cross_kernel(
@@ -41,130 +42,160 @@ def tile_list_auction_lowrank_cross_kernel(
         def bank(b, shape):
             return psum.tile(shape, F32, name=f"bank{b}")
 
+        def held(shape, dtype, name):
+            return keep.tile(shape, dtype, name=name, align_bytes=64)
+
         gather_offs = keep.tile([P, S // 16], U16, name="gather_offs")
         scatter_offs = keep.tile([P, S // 16], U16, name="scatter_offs")
-        tab_s = keep.tile([P, T], U8, name="tab_s", align_bytes=64)
-        v_w = [keep.tile([P, S], U32, name=f"v_w{a}", align_bytes=64) for a in range(PASSES)]
-        v_s = [keep.tile([P, HALF], U8, name="v_s", align_bytes=64)]
-        w1_raw = [keep.tile([P, PACK, R], F32, name=f"w1_raw{a}", align_bytes=64) for a in range(PASSES)]
-        w1_bf = [keep.tile([P, PACK * R], BF16, name=f"w1_bf{a}", align_bytes=64) for a in range(PASSES)]
-        w1_w = [keep.tile([P, R], U32, name=f"w1_w{a}", align_bytes=64) for a in range(PASSES)]
-        w1_s = [keep.tile([P, R], U8, name=f"w1_s{a}", align_bytes=64) for a in range(PASSES)]
-        wx_s = keep.tile([P, N], U8, name="wx_s", align_bytes=64)
-        wu_s = keep.tile([P, N], U8, name="wu_s", align_bytes=64)
-        h_bf = keep.tile([P, PACK * S], BF16, name="h_bf", align_bytes=64)
-        h_w = keep.tile([P, S], U32, name="h_w", align_bytes=64)
-        h_s = keep.tile([P, S], U8, name="h_s", align_bytes=64)
-        b2_rows = keep.tile([P, P], F32, name="b2_rows", align_bytes=64)
-        ident = keep.tile([P, P], F32, name="ident", align_bytes=64)
+        tab_s = held([P, T], U8, "tab_s")
+        tab_w = [held([P, T], I32, f"tab_w{a}") for a in range(PASSES)]
+        v_s = held([P, S], U8, "v_s")
+        v_w = [held([P, S], U32, f"v_w{a}") for a in range(PASSES)]
+        w1_raw = [held([P, PACK, R], F32, f"w1_raw{a}") for a in range(PASSES)]
+        w1_bf = [held([P, PACK * R], BF16, f"w1_bf{a}") for a in range(PASSES)]
+        w1_w = [held([P, R], U32, f"w1_w{a}") for a in range(PASSES)]
+        w1_s = [held([P, R], U8, f"w1_s{a}") for a in range(PASSES)]
+        w_s = held([P, N], U8, "w_s")
+        h_w = held([P, S], U32, "h_w")
+        h_s = held([P, S], U8, "h_s")
+        b2_rows = held([P, P], F32, "b2_rows")
+        ident = held([P, P], F32, "ident")
         bias = keep.tile([P, TILES], F32, name="bias")
-        cache = [keep.tile([P, T2], F32, name=f"cache{b}", align_bytes=64) for b in range(2)]
+        cache = [held([P, T2], F32, f"cache{b}") for b in range(2)]
 
-        for plane in (tab_s, wx_s, wu_s):
-            nc.vector.memset(plane[:].bitcast(I32), 0)
+        for plane in (tab_s, w_s):
+            nc.gpsimd.memset(plane[:].bitcast(I32), 0)
+        make_identity(nc, ident[:])
 
-        def load_scales(queue, plane, src, passes):
+        def load_scales(queue, plane, row, src, passes):
             for q in range(4):
-                queue.dma_start(
-                    plane[32 * q : 32 * q + 4 * passes, :].bitcast(I32), src[:, 4 * q : 4 * q + 4, :].bitcast(I32)
-                )
+                rows = plane[32 * q + row : 32 * q + row + 4 * passes, :]
+                queue.dma_start(rows.bitcast(I32), src[:, 4 * q : 4 * q + 4, :].bitcast(I32))
 
+        def load_w1(a):
+            rows = w1[P * PACK * a : P * PACK * (a + 1), :]
+            nc.sync.dma_start(w1_raw[a][:], rows.rearrange("(p j) r -> p j r", j=PACK))
+
+        def load_table(a):
+            nc.sync.dma_start(tab_w[a][:], tab_words[a].rearrange("p t i -> p (t i)").bitcast(I32))
+
+        nc.sync.dma_start(gather_offs[:], offs)
         nc.sync.dma_start(
             b2_rows[:], b2.rearrange("(i p) -> i p", p=P).unsqueeze(0).broadcast_to([P // TILES, TILES, P])
         )
-        nc.sync.dma_start(gather_offs[:], offs)
-        for a in range(PASSES):
-            rows = w1[P * PACK * a : P * PACK * (a + 1), :]
-            nc.sync.dma_start(w1_raw[a][:], rows.rearrange("(p j) r -> p j r", j=PACK))
         nc.sync.dma_start(scatter_offs[:], offs2)
-        load_scales(nc.sync, tab_s, tab_scales, PASSES)
+        load_w1(0)
+        load_scales(nc.sync, tab_s, 0, tab_scales, PASSES)
+        load_table(0)
+        load_scales(nc.sync, w_s, 0, wu_scales, 1)
+        load_w1(1)
+        load_table(1)
+        load_scales(nc.gpsimd, w_s, WX_ROW, wx_scales, PASSES)
 
-        make_identity(nc, ident[:])
         b2_cols = bank(7, [P, P])
         nc.tensor.transpose(b2_cols[:], b2_rows[:], ident[:])
         nc.scalar.activation(bias[:], b2_cols[:, 0:TILES], ACT.Copy, bias=1.0)
 
-        tab_w = [keep.tile([P, T], I32, name=name, align_bytes=64) for name in ("ident", "b2_rows")]
-        for a in range(PASSES):
-            nc.sync.dma_start(tab_w[a][:], tab_words[a].rearrange("p t i -> p (t i)").bitcast(I32))
-        load_scales(nc.gpsimd, wx_s, wx_scales, PASSES)
-        load_scales(nc.gpsimd, wu_s, wu_scales, 1)
+        wx_src = wx_words.rearrange("a p e i -> p a (e i)").bitcast(I32)
+        wx_first = held([P, PASSES, FIRST_TILES * P], I32, "b2_rows")
+        nc.sync.dma_start(wx_first[:], wx_src[:, :, 0 : FIRST_TILES * P])
+        wgo_sb = held([P, S], F32, "ident")
+        nc.sync.dma_start(wgo_sb[:, 0:HALF], wgo[:, 0:HALF])
 
         for tile in cache:
-            nc.vector.memset(tile[:, 0 : T2 // 2], 0.0)
-            nc.vector.memset(tile[:, T2 // 2 : T2], 0.0)
+            nc.vector.memset(tile[:], 0.0)
 
-        for a in range(PASSES):
+        def cast_views(a):
             dst = w1_bf[a][:].rearrange("p (t m j) -> p m t j", t=PACK, j=PACK)
-            src = w1_raw[a][:].rearrange("p j (m t) -> p m t j", t=PACK)
-            nc.vector.tensor_copy(dst[:, 0:CAST_SPLIT], src[:, 0:CAST_SPLIT])
-            nc.scalar.copy(dst[:, CAST_SPLIT:P], src[:, CAST_SPLIT:P])
+            return dst, w1_raw[a][:].rearrange("p j (m t) -> p m t j", t=PACK)
+
+        def quantize_w1(a):
             nc.vector.quantize_mx(out=w1_w[a][:].bitcast(FP8X4), scales=w1_s[a][:], in_=w1_bf[a][:])
 
-        wx_src = wx_words.rearrange("a p e i -> p a (e i)").bitcast(I32)
-        wx_first = keep.tile([P, PASSES, P], I32, name="w1_raw0", align_bytes=64)
-        nc.sync.dma_start(wx_first[:], wx_src[:, :, 0:P])
-        wgo_sb = keep.tile([P, S], F32, name="w1_bf0", align_bytes=64)
-        nc.sync.dma_start(wgo_sb[:], wgo)
-        wu_w = keep.tile([P, 2 * N], U8, name="w1_raw1", align_bytes=64)
+        def gather_words(a):
+            for lo, hi in ((0, QUARTER), (QUARTER, HALF), (HALF, S)):
+                window = tab_w[a][:].bitcast(U32).indirect(gather_offs[:, lo // 16 : hi // 16])
+                nc.vector.tensor_copy(v_w[a][:, lo:hi], window)
+
+        def cast_w1(a):
+            dst, src = cast_views(a)
+            nc.vector.tensor_copy(dst[:, 0:CAST_SPLIT], src[:, 0:CAST_SPLIT])
+            nc.scalar.copy(dst[:, CAST_SPLIT:P], src[:, CAST_SPLIT:P])
+
+        nc.scalar.copy(*cast_views(0))
+        nc.vector.tensor_copy(v_s[:], tab_s[:].indirect(gather_offs[:]))
+        quantize_w1(0)
+        wu_w = held([P, 2 * N], U8, "w1_raw0")
         nc.sync.dma_start(wu_w[:].bitcast(I32), wu_words[0].bitcast(I32))
-        wx_rest = keep.tile([P, PASSES, N - P], I32, name="w1_bf1", align_bytes=64)
-        nc.sync.dma_start(wx_rest[:], wx_src[:, :, P:N])
+        nc.sync.dma_start(wgo_sb[:, HALF:S], wgo[:, HALF:S])
+        gather_words(0)
+        wx_rest = held([P, PASSES, N - FIRST_TILES * P], I32, "tab_w0")
+        nc.sync.dma_start(wx_rest[:], wx_src[:, :, FIRST_TILES * P : N])
+        cast_w1(1)
+        quantize_w1(1)
+        cache.append(held([P, T2], F32, "w1_bf1"))
+        nc.gpsimd.memset(cache[2][:], 0.0)
+        gather_words(1)
 
-        def v_plane(a, lo, hi):
-            return v_s[lo // HALF][4 * a : P, lo % HALF : lo % HALF + hi - lo]
+        h_bf = [held([P, PACK * QUARTER], BF16, "h_bf0"), held([P, PACK * QUARTER], BF16, "h_bf1")]
+        h_bf.append(held([P, PACK * HALF], BF16, "h_bf2"))
 
-        def gather_scales(lo, hi):
-            nc.vector.tensor_copy(v_plane(0, lo, hi), tab_s[:].indirect(gather_offs[:, lo // 16 : hi // 16]))
-
-        def gather_words(a, lo, hi):
-            window = tab_w[a][:].bitcast(U32).indirect(gather_offs[:, lo // 16 : hi // 16])
-            nc.vector.tensor_copy(v_w[a][:, lo:hi], window)
-
-        def rank_space(lo, hi):
-            for g in range(lo // GROUP, hi // GROUP):
-                acc = bank(H_BANKS[g], [P, PACK, GROUP])
-                for t in range(PACK):
-                    for a in range(PASSES):
-                        nc.tensor.matmul_mx(
-                            out=acc[:, t, :],
-                            lhsT=w1_w[a][:, t * P : (t + 1) * P].bitcast(FP8X4),
-                            lhsT_scale=w1_s[a][:, t * P : (t + 1) * P],
-                            rhs=v_w[a][:, g * GROUP : (g + 1) * GROUP].bitcast(FP8X4),
-                            rhs_scale=v_plane(a, g * GROUP, (g + 1) * GROUP),
-                            start=(a == 0),
-                            stop=(a == PASSES - 1),
-                        )
-                nc.scalar.activation(
-                    h_bf[:, PACK * g * GROUP : PACK * (g + 1) * GROUP].rearrange("p (j t) -> p j t", t=PACK),
-                    acc[:].rearrange("p t j -> p j t"),
-                    ACT.Relu,
+        def h_pass(acc, g, a):
+            lo, hi = g * GROUP, (g + 1) * GROUP
+            for t in range(PACK):
+                nc.tensor.matmul_mx(
+                    out=acc[:, t, :],
+                    lhsT=w1_w[a][:, t * P : (t + 1) * P].bitcast(FP8X4),
+                    lhsT_scale=w1_s[a][:, t * P : (t + 1) * P],
+                    rhs=v_w[a][:, lo:hi].bitcast(FP8X4),
+                    rhs_scale=v_s[4 * a : P, lo:hi],
+                    start=(a == 0 and t == 0),
+                    stop=(a == PASSES - 1 and t == PACK - 1),
                 )
-            nc.vector.quantize_mx(
-                out=h_w[:, lo:hi].bitcast(FP8X4), scales=h_s[:, lo:hi], in_=h_bf[:, PACK * lo : PACK * hi]
+
+        def relu(acc, dst, k):
+            nc.scalar.activation(
+                dst[:, PACK * k * GROUP : PACK * (k + 1) * GROUP].rearrange("p (j t) -> p j t", t=PACK),
+                acc[:].rearrange("p t j -> p j t"),
+                ACT.Relu,
             )
 
-        def weighted_x(i, lo, hi, b, x_sb, xw_sb):
-            acc = bank(b, [P, hi - lo])
+        def quantize_h(src, lo, hi):
+            nc.vector.quantize_mx(out=h_w[:, lo:hi].bitcast(FP8X4), scales=h_s[:, lo:hi], in_=src[:])
+
+        def x_pass(acc, i, a, lo, hi, start, stop):
+            wx_w = wx_first[:, a, i * P : (i + 1) * P] if i < FIRST_TILES else (
+                wx_rest[:, a, (i - FIRST_TILES) * P : (i - FIRST_TILES + 1) * P]
+            )
+            nc.tensor.matmul_mx(
+                out=acc,
+                lhsT=wx_w.bitcast(FP8X4),
+                lhsT_scale=w_s[WX_ROW + 4 * a : P, i * P : (i + 1) * P],
+                rhs=v_w[a][:, lo:hi].bitcast(FP8X4),
+                rhs_scale=v_s[4 * a : P, lo:hi],
+                start=start,
+                stop=stop,
+            )
+
+        def x_half(i, c, b):
+            acc = bank(b, [P, HALF])
+            lo = c * HALF
             for a in range(PASSES):
-                nc.tensor.matmul_mx(
-                    out=acc[:],
-                    lhsT=(wx_first[:, a, :] if i == 0 else wx_rest[:, a, (i - 1) * P : i * P]).bitcast(FP8X4),
-                    lhsT_scale=wx_s[4 * a : P, i * P : (i + 1) * P],
-                    rhs=v_w[a][:, lo:hi].bitcast(FP8X4),
-                    rhs_scale=v_plane(a, lo, hi),
-                    start=(a == 0),
-                    stop=(a == PASSES - 1),
-                )
+                x_pass(acc[:], i, a, lo, lo + HALF, a == 0, a == PASSES - 1)
+            return acc
+
+        def weighted_x(i, c, b, xw_sb):
+            acc = x_half(i, c, b)
+            x_sb = ring.tile([P, HALF], F32, name="x_sb", align_bytes=64, bufs=3)
             nc.scalar.copy(x_sb[:], acc[:])
-            nc.gpsimd.tensor_tensor(xw_sb[:, lo:hi], x_sb[:], wgo_sb[:, lo:hi], MULT)
+            nc.gpsimd.tensor_tensor(xw_sb[:, c * HALF : (c + 1) * HALF], x_sb[:], wgo_sb[:, c * HALF : (c + 1) * HALF], MULT)
 
         def cross(i, lo, hi, b):
             acc = bank(b, [P, hi - lo])
             nc.tensor.matmul_mx(
                 out=acc[:],
                 lhsT=wu_w[:, 2 * i * P : 2 * (i + 1) * P].bitcast(FP4X4),
-                lhsT_scale=wu_s[:, i * P : (i + 1) * P],
+                lhsT_scale=w_s[:, i * P : (i + 1) * P],
                 rhs=h_w[:, lo:hi].bitcast(FP8X4),
                 rhs_scale=h_s[:, lo:hi],
                 start=True,
@@ -182,45 +213,64 @@ def tile_list_auction_lowrank_cross_kernel(
             nc.scalar.activation(c_sb[:], acc[:], ACT.Identity, bias=bias[:, i : i + 1])
             nc.gpsimd.tensor_tensor(y_sb[:, lo:hi], xw_sb[:, lo:hi], c_sb[:], MULT)
 
-        def x_tile(width):
-            return ring.tile([P, width], F32, name="x_sb", align_bytes=64, bufs=3)
-
         def scatter(i, lo, hi, y_sb):
-            window = cache[i % 2][:].indirect(scatter_offs[:, lo // 16 : hi // 16])
+            window = cache[i % 3][:].indirect(scatter_offs[:, lo // 16 : hi // 16])
             nc.vector.tensor_copy(window, y_sb[:, lo:hi])
 
         xw_sb = ring.tile([P, S], F32, name="xw_sb", align_bytes=64)
         y_sb = ring.tile([P, S], F32, name="y_sb", align_bytes=64, bufs=3)
-        gather_scales(0, HALF)
-        gather_words(0, 0, HALF)
-        gather_words(1, 0, QUARTER)
-        weighted_x(0, 0, QUARTER, 2, keep.tile([P, QUARTER], F32, name="x_first", align_bytes=64), xw_sb)
-        v_s.append(keep.tile([P, HALF], U8, name="x_first", align_bytes=64))
-        rank_space(0, QUARTER)
-        finish_on_vector(0, 0, QUARTER, 4, xw_sb, y_sb)
-        gather_words(1, QUARTER, HALF)
-        rank_space(QUARTER, HALF)
-        weighted_x(0, QUARTER, HALF, 3, x_tile(QUARTER), xw_sb)
-        finish_on_vector(0, QUARTER, HALF, 5, xw_sb, y_sb)
-        gather_scales(HALF, S)
-        for a in range(PASSES):
-            gather_words(a, HALF, S)
-        rank_space(HALF, S)
-        weighted_x(0, HALF, S, 2, x_tile(HALF), xw_sb)
-        finish_on_vector(0, HALF, S, 6, xw_sb, y_sb)
-        for lo, hi in ((0, QUARTER), (QUARTER, HALF), (HALF, S)):
-            scatter(0, lo, hi, y_sb)
-        nc.sync.dma_start(out[0:P, :], cache[0][:])
+        accs = [bank(b, [P, PACK, GROUP]) for b in (0, 1, 2, 3, 5, 6)]
+        for g in range(6):
+            h_pass(accs[g], g, 0)
+        for g in range(2):
+            h_pass(accs[g], g, 1)
+            relu(accs[g], h_bf[0], g)
+        x_acc = x_half(0, 0, 4)
+        quantize_h(h_bf[0], 0, QUARTER)
+        for lo in (0, QUARTER):
+            cols = slice(lo, lo + QUARTER)
+            nc.vector.tensor_tensor(xw_sb[:, cols], x_acc[:, cols], wgo_sb[:, cols], MULT)
+        for g in range(2, 4):
+            h_pass(accs[g], g, 1)
+            relu(accs[g], h_bf[1], g - 2)
+        finish_on_vector(0, 0, QUARTER, 7, xw_sb, y_sb)
+        quantize_h(h_bf[1], QUARTER, HALF)
+        scatter(0, 0, QUARTER, y_sb)
+        for g in range(4, 6):
+            h_pass(accs[g], g, 1)
+            relu(accs[g], h_bf[2], g - 4)
+        xw_next = ring.tile([P, S], F32, name="xw_sb", align_bytes=64)
+        y_next = ring.tile([P, S], F32, name="y_sb", align_bytes=64, bufs=3)
+        for g in range(6, 8):
+            acc = bank(g - 6, [P, PACK, GROUP])
+            for a in range(PASSES):
+                h_pass(acc, g, a)
+            relu(acc, h_bf[2], g - 4)
+            if g == 6:
+                weighted_x(1, 0, 5, xw_next)
+        finish_on_vector(0, QUARTER, HALF, 0, xw_sb, y_sb)
+        quantize_h(h_bf[2], HALF, S)
+        scatter(0, QUARTER, HALF, y_sb)
+        finish_on_gpsimd(1, 0, HALF, 6, xw_next, y_next)
+        scatter(1, 0, HALF, y_next)
+        for i, xw, y, x_bank, c_bank in ((0, xw_sb, y_sb, 2, 3), (1, xw_next, y_next, 4, 7)):
+            weighted_x(i, 1, x_bank, xw)
+            finish_on_gpsimd(i, HALF, S, c_bank, xw, y)
+            scatter(i, HALF, S, y)
+            nc.sync.dma_start(out[i * P : (i + 1) * P, :], cache[i][:])
 
-        for i in range(1, TILES):
+        for i in range(2, TILES):
+            x_sb = ring.tile([P, S], F32, name="x_sb", align_bytes=64, bufs=3)
+            c_sb = ring.tile([P, S], F32, name="c_sb", align_bytes=64, bufs=3)
             xw_sb = ring.tile([P, S], F32, name="xw_sb", align_bytes=64)
             y_sb = ring.tile([P, S], F32, name="y_sb", align_bytes=64, bufs=3)
-            x_banks, c_banks = ((2, 3), (0, 1)) if i % 2 else ((4, 5), (6, 7))
+            x_banks, c_banks = ((2, 4), (3, 7)) if i % 2 else ((0, 1), (5, 6))
             for c in range(2):
-                weighted_x(i, c * HALF, (c + 1) * HALF, x_banks[c], x_tile(HALF), xw_sb)
-                finish_on_gpsimd(i, c * HALF, (c + 1) * HALF, c_banks[c], xw_sb, y_sb)
-                if i == 1:
-                    scatter(i, c * HALF, (c + 1) * HALF, y_sb)
-            if i > 1:
-                scatter(i, 0, S, y_sb)
-            nc.sync.dma_start(out[i * P : (i + 1) * P, :], cache[i % 2][:])
+                nc.scalar.copy(x_sb[:, c * HALF : (c + 1) * HALF], x_half(i, c, x_banks[c])[:])
+            nc.gpsimd.tensor_tensor(xw_sb[:], x_sb[:], wgo_sb[:], MULT)
+            for c in range(2):
+                acc = cross(i, c * HALF, (c + 1) * HALF, c_banks[c])
+                nc.scalar.activation(c_sb[:, c * HALF : (c + 1) * HALF], acc[:], ACT.Identity, bias=bias[:, i : i + 1])
+            nc.gpsimd.tensor_tensor(y_sb[:], xw_sb[:], c_sb[:], MULT)
+            scatter(i, 0, S, y_sb)
+            nc.sync.dma_start(out[i * P : (i + 1) * P, :], cache[i % 3][:])

@@ -25,7 +25,7 @@ TILES = N // P
 HALF = 512
 QUARTER = 256
 GROUP = 128
-CAST_SPLIT = 32
+CAST_SPLIT = 64
 WX_ROW = 4
 FIRST_TILES = 2
 
@@ -61,7 +61,7 @@ def tile_list_auction_lowrank_cross_kernel(
         b2_rows = held([P, P], F32, "b2_rows")
         ident = held([P, P], F32, "ident")
         bias = keep.tile([P, TILES], F32, name="bias")
-        cache = [held([P, T2], F32, f"cache{b}") for b in range(2)]
+        cache = [held([P, T2], F32, f"cache{b}") for b in range(3)]
 
         for plane in (tab_s, w_s):
             nc.gpsimd.memset(plane[:].bitcast(I32), 0)
@@ -133,8 +133,6 @@ def tile_list_auction_lowrank_cross_kernel(
         nc.sync.dma_start(wx_rest[:], wx_src[:, :, FIRST_TILES * P : N])
         cast_w1(1)
         quantize_w1(1)
-        cache.append(held([P, T2], F32, "w1_bf1"))
-        nc.gpsimd.memset(cache[2][:], 0.0)
         gather_words(1)
 
         h_bf = [held([P, PACK * QUARTER], BF16, "h_bf0"), held([P, PACK * QUARTER], BF16, "h_bf1")]
@@ -241,13 +239,12 @@ def tile_list_auction_lowrank_cross_kernel(
             relu(accs[g], h_bf[2], g - 4)
         xw_next = ring.tile([P, S], F32, name="xw_sb", align_bytes=64)
         y_next = ring.tile([P, S], F32, name="y_sb", align_bytes=64, bufs=3)
+        weighted_x(1, 0, 5, xw_next)
         for g in range(6, 8):
             acc = bank(g - 6, [P, PACK, GROUP])
             for a in range(PASSES):
                 h_pass(acc, g, a)
             relu(acc, h_bf[2], g - 4)
-            if g == 6:
-                weighted_x(1, 0, 5, xw_next)
         finish_on_vector(0, QUARTER, HALF, 0, xw_sb, y_sb)
         quantize_h(h_bf[2], HALF, S)
         scatter(0, QUARTER, HALF, y_sb)

@@ -26,7 +26,7 @@ HALF = 512
 QUARTER = 256
 GROUP = 128
 CAST_SPLIT = 64
-WX_ROW = 4
+ODD_SPLIT = 1023
 FIRST_TILES = 2
 
 
@@ -55,21 +55,21 @@ def tile_list_auction_lowrank_cross_kernel(
         w1_bf = [held([P, PACK * R], BF16, f"w1_bf{a}") for a in range(PASSES)]
         w1_w = [held([P, R], U32, f"w1_w{a}") for a in range(PASSES)]
         w1_s = [held([P, R], U8, f"w1_s{a}") for a in range(PASSES)]
-        w_s = held([P, N], U8, "w_s")
+        wx_s = held([P, N], U8, "wx_s")
+        wu_s = held([P, N], U8, "wu_s")
         h_w = held([P, S], U32, "h_w")
         h_s = held([P, S], U8, "h_s")
         b2_rows = held([P, P], F32, "b2_rows")
         ident = held([P, P], F32, "ident")
-        bias = keep.tile([P, TILES], F32, name="bias")
         cache = [held([P, T2], F32, f"cache{b}") for b in range(3)]
 
-        for plane in (tab_s, w_s):
+        for plane in (tab_s, wx_s, wu_s):
             nc.gpsimd.memset(plane[:].bitcast(I32), 0)
         make_identity(nc, ident[:])
 
-        def load_scales(queue, plane, row, src, passes):
+        def load_scales(queue, plane, src, passes):
             for q in range(4):
-                rows = plane[32 * q + row : 32 * q + row + 4 * passes, :]
+                rows = plane[32 * q : 32 * q + 4 * passes, :]
                 queue.dma_start(rows.bitcast(I32), src[:, 4 * q : 4 * q + 4, :].bitcast(I32))
 
         def load_w1(a):
@@ -79,22 +79,21 @@ def tile_list_auction_lowrank_cross_kernel(
         def load_table(a):
             nc.sync.dma_start(tab_w[a][:], tab_words[a].rearrange("p t i -> p (t i)").bitcast(I32))
 
+        load_w1(0)
         nc.sync.dma_start(gather_offs[:], offs)
         nc.sync.dma_start(
             b2_rows[:], b2.rearrange("(i p) -> i p", p=P).unsqueeze(0).broadcast_to([P // TILES, TILES, P])
         )
-        nc.sync.dma_start(scatter_offs[:], offs2)
-        load_w1(0)
-        load_scales(nc.sync, tab_s, 0, tab_scales, PASSES)
+        load_scales(nc.sync, tab_s, tab_scales, PASSES)
         load_table(0)
-        load_scales(nc.sync, w_s, 0, wu_scales, 1)
         load_w1(1)
         load_table(1)
-        load_scales(nc.gpsimd, w_s, WX_ROW, wx_scales, PASSES)
+        nc.sync.dma_start(scatter_offs[:], offs2)
+        load_scales(nc.gpsimd, wx_s, wx_scales, PASSES)
+        load_scales(nc.gpsimd, wu_s, wu_scales, 1)
 
         b2_cols = bank(7, [P, P])
         nc.tensor.transpose(b2_cols[:], b2_rows[:], ident[:])
-        nc.scalar.activation(bias[:], b2_cols[:, 0:TILES], ACT.Copy, bias=1.0)
 
         wx_src = wx_words.rearrange("a p e i -> p a (e i)").bitcast(I32)
         wx_first = held([P, PASSES, FIRST_TILES * P], I32, "b2_rows")
@@ -102,7 +101,9 @@ def tile_list_auction_lowrank_cross_kernel(
         wgo_sb = held([P, S], F32, "ident")
         nc.sync.dma_start(wgo_sb[:, 0:HALF], wgo[:, 0:HALF])
 
-        for tile in cache:
+        nc.vector.memset(cache[0][:, 0:ODD_SPLIT], 0.0)
+        nc.vector.memset(cache[0][:, ODD_SPLIT:T2], 0.0)
+        for tile in cache[1:]:
             nc.vector.memset(tile[:], 0.0)
 
         def cast_views(a):
@@ -123,9 +124,11 @@ def tile_list_auction_lowrank_cross_kernel(
             nc.scalar.copy(dst[:, CAST_SPLIT:P], src[:, CAST_SPLIT:P])
 
         nc.scalar.copy(*cast_views(0))
+        bias = held([P, TILES], F32, "w1_raw0")
+        nc.scalar.activation(bias[:], b2_cols[:, 0:TILES], ACT.Copy, bias=1.0)
         nc.vector.tensor_copy(v_s[:], tab_s[:].indirect(gather_offs[:]))
         quantize_w1(0)
-        wu_w = held([P, 2 * N], U8, "w1_raw0")
+        wu_w = held([P, 2 * N], U8, "tab_s")
         nc.sync.dma_start(wu_w[:].bitcast(I32), wu_words[0].bitcast(I32))
         nc.sync.dma_start(wgo_sb[:, HALF:S], wgo[:, HALF:S])
         gather_words(0)
@@ -168,7 +171,7 @@ def tile_list_auction_lowrank_cross_kernel(
             nc.tensor.matmul_mx(
                 out=acc,
                 lhsT=wx_w.bitcast(FP8X4),
-                lhsT_scale=w_s[WX_ROW + 4 * a : P, i * P : (i + 1) * P],
+                lhsT_scale=wx_s[4 * a : P, i * P : (i + 1) * P],
                 rhs=v_w[a][:, lo:hi].bitcast(FP8X4),
                 rhs_scale=v_s[4 * a : P, lo:hi],
                 start=start,
@@ -193,7 +196,7 @@ def tile_list_auction_lowrank_cross_kernel(
             nc.tensor.matmul_mx(
                 out=acc[:],
                 lhsT=wu_w[:, 2 * i * P : 2 * (i + 1) * P].bitcast(FP4X4),
-                lhsT_scale=w_s[:, i * P : (i + 1) * P],
+                lhsT_scale=wu_s[:, i * P : (i + 1) * P],
                 rhs=h_w[:, lo:hi].bitcast(FP8X4),
                 rhs_scale=h_s[:, lo:hi],
                 start=True,

@@ -27,6 +27,7 @@ QUARTER = 256
 GROUP = 128
 CAST_SPLIT = 64
 ODD_SPLIT = 1023
+V_ROW, WX_ROW = 4, 8
 FIRST_TILES = 2
 
 
@@ -61,15 +62,16 @@ def tile_list_auction_lowrank_cross_kernel(
         h_s = held([P, S], U8, "h_s")
         b2_rows = held([P, P], F32, "b2_rows")
         ident = held([P, P], F32, "ident")
-        cache = [held([P, T2], F32, f"cache{b}") for b in range(3)]
+        cache = [held([P, T2], F32, f"cache{b}") for b in range(2)]
 
-        for plane in (tab_s, wx_s, wu_s):
-            nc.gpsimd.memset(plane[:].bitcast(I32), 0)
+        nc.gpsimd.memset(tab_s[:].bitcast(I32), 0)
         make_identity(nc, ident[:])
+        for plane in (wx_s, wu_s):
+            nc.vector.memset(plane[:].bitcast(I32), 0)
 
-        def load_scales(queue, plane, src, passes):
+        def load_scales(queue, plane, row, src, passes):
             for q in range(4):
-                rows = plane[32 * q : 32 * q + 4 * passes, :]
+                rows = plane[32 * q + row : 32 * q + row + 4 * passes, :]
                 queue.dma_start(rows.bitcast(I32), src[:, 4 * q : 4 * q + 4, :].bitcast(I32))
 
         def load_w1(a):
@@ -84,13 +86,13 @@ def tile_list_auction_lowrank_cross_kernel(
         nc.sync.dma_start(
             b2_rows[:], b2.rearrange("(i p) -> i p", p=P).unsqueeze(0).broadcast_to([P // TILES, TILES, P])
         )
-        load_scales(nc.sync, tab_s, tab_scales, PASSES)
+        load_scales(nc.sync, tab_s, V_ROW, tab_scales, PASSES)
         load_table(0)
         load_w1(1)
         load_table(1)
         nc.sync.dma_start(scatter_offs[:], offs2)
-        load_scales(nc.gpsimd, wx_s, wx_scales, PASSES)
-        load_scales(nc.gpsimd, wu_s, wu_scales, 1)
+        load_scales(nc.gpsimd, wx_s, WX_ROW, wx_scales, PASSES)
+        load_scales(nc.gpsimd, wu_s, 0, wu_scales, 1)
 
         b2_cols = bank(7, [P, P])
         nc.tensor.transpose(b2_cols[:], b2_rows[:], ident[:])
@@ -101,10 +103,9 @@ def tile_list_auction_lowrank_cross_kernel(
         wgo_sb = held([P, S], F32, "ident")
         nc.sync.dma_start(wgo_sb[:, 0:HALF], wgo[:, 0:HALF])
 
-        nc.vector.memset(cache[0][:, 0:ODD_SPLIT], 0.0)
-        nc.vector.memset(cache[0][:, ODD_SPLIT:T2], 0.0)
-        for tile in cache[1:]:
-            nc.vector.memset(tile[:], 0.0)
+        for tile in cache:
+            nc.vector.memset(tile[:, 0:ODD_SPLIT], 0.0)
+            nc.vector.memset(tile[:, ODD_SPLIT:T2], 0.0)
 
         def cast_views(a):
             dst = w1_bf[a][:].rearrange("p (t m j) -> p m t j", t=PACK, j=PACK)
@@ -136,6 +137,8 @@ def tile_list_auction_lowrank_cross_kernel(
         nc.sync.dma_start(wx_rest[:], wx_src[:, :, FIRST_TILES * P : N])
         cast_w1(1)
         quantize_w1(1)
+        cache.append(held([P, T2], F32, "w1_bf1"))
+        nc.gpsimd.memset(cache[2][:], 0.0)
         gather_words(1)
 
         h_bf = [held([P, PACK * QUARTER], BF16, "h_bf0"), held([P, PACK * QUARTER], BF16, "h_bf1")]
@@ -149,7 +152,7 @@ def tile_list_auction_lowrank_cross_kernel(
                     lhsT=w1_w[a][:, t * P : (t + 1) * P].bitcast(FP8X4),
                     lhsT_scale=w1_s[a][:, t * P : (t + 1) * P],
                     rhs=v_w[a][:, lo:hi].bitcast(FP8X4),
-                    rhs_scale=v_s[4 * a : P, lo:hi],
+                    rhs_scale=v_s[V_ROW + 4 * a : P, lo:hi],
                     start=(a == 0 and t == 0),
                     stop=(a == PASSES - 1 and t == PACK - 1),
                 )
@@ -171,9 +174,9 @@ def tile_list_auction_lowrank_cross_kernel(
             nc.tensor.matmul_mx(
                 out=acc,
                 lhsT=wx_w.bitcast(FP8X4),
-                lhsT_scale=wx_s[4 * a : P, i * P : (i + 1) * P],
+                lhsT_scale=wx_s[WX_ROW + 4 * a : P, i * P : (i + 1) * P],
                 rhs=v_w[a][:, lo:hi].bitcast(FP8X4),
-                rhs_scale=v_s[4 * a : P, lo:hi],
+                rhs_scale=v_s[V_ROW + 4 * a : P, lo:hi],
                 start=start,
                 stop=stop,
             )
@@ -226,14 +229,14 @@ def tile_list_auction_lowrank_cross_kernel(
         for g in range(2):
             h_pass(accs[g], g, 1)
             relu(accs[g], h_bf[0], g)
-        x_acc = x_half(0, 0, 4)
         quantize_h(h_bf[0], 0, QUARTER)
-        for lo in (0, QUARTER):
-            cols = slice(lo, lo + QUARTER)
-            nc.vector.tensor_tensor(xw_sb[:, cols], x_acc[:, cols], wgo_sb[:, cols], MULT)
         for g in range(2, 4):
             h_pass(accs[g], g, 1)
             relu(accs[g], h_bf[1], g - 2)
+        x_acc = x_half(0, 0, 4)
+        for lo in (0, QUARTER):
+            cols = slice(lo, lo + QUARTER)
+            nc.vector.tensor_tensor(xw_sb[:, cols], x_acc[:, cols], wgo_sb[:, cols], MULT)
         finish_on_vector(0, 0, QUARTER, 7, xw_sb, y_sb)
         quantize_h(h_bf[1], QUARTER, HALF)
         scatter(0, 0, QUARTER, y_sb)

@@ -62,12 +62,11 @@ def tile_list_auction_lowrank_cross_kernel(
         h_s = held([P, S], U8, "h_s")
         b2_rows = held([P, P], F32, "b2_rows")
         ident = held([P, P], F32, "ident")
-        cache = [held([P, T2], F32, f"cache{b}") for b in range(2)]
+        cache = [held([P, T2], F32, f"cache{b}") for b in range(3)]
 
-        nc.gpsimd.memset(tab_s[:].bitcast(I32), 0)
+        for plane in (tab_s, wu_s, wx_s):
+            nc.gpsimd.memset(plane[:].bitcast(I32), 0)
         make_identity(nc, ident[:])
-        for plane in (wx_s, wu_s):
-            nc.vector.memset(plane[:].bitcast(I32), 0)
 
         def load_scales(queue, plane, row, src, passes):
             for q in range(4):
@@ -88,11 +87,11 @@ def tile_list_auction_lowrank_cross_kernel(
         )
         load_scales(nc.sync, tab_s, V_ROW, tab_scales, PASSES)
         load_table(0)
+        load_scales(nc.sync, wu_s, 0, wu_scales, 1)
         load_w1(1)
         load_table(1)
         nc.sync.dma_start(scatter_offs[:], offs2)
         load_scales(nc.gpsimd, wx_s, WX_ROW, wx_scales, PASSES)
-        load_scales(nc.gpsimd, wu_s, 0, wu_scales, 1)
 
         b2_cols = bank(7, [P, P])
         nc.tensor.transpose(b2_cols[:], b2_rows[:], ident[:])
@@ -103,9 +102,10 @@ def tile_list_auction_lowrank_cross_kernel(
         wgo_sb = held([P, S], F32, "ident")
         nc.sync.dma_start(wgo_sb[:, 0:HALF], wgo[:, 0:HALF])
 
-        for tile in cache:
-            nc.vector.memset(tile[:, 0:ODD_SPLIT], 0.0)
-            nc.vector.memset(tile[:, ODD_SPLIT:T2], 0.0)
+        nc.vector.memset(cache[0][:, 0:ODD_SPLIT], 0.0)
+        nc.vector.memset(cache[0][:, ODD_SPLIT:T2], 0.0)
+        for tile in cache[1:]:
+            nc.vector.memset(tile[:], 0.0)
 
         def cast_views(a):
             dst = w1_bf[a][:].rearrange("p (t m j) -> p m t j", t=PACK, j=PACK)
@@ -137,8 +137,6 @@ def tile_list_auction_lowrank_cross_kernel(
         nc.sync.dma_start(wx_rest[:], wx_src[:, :, FIRST_TILES * P : N])
         cast_w1(1)
         quantize_w1(1)
-        cache.append(held([P, T2], F32, "w1_bf1"))
-        nc.gpsimd.memset(cache[2][:], 0.0)
         gather_words(1)
 
         h_bf = [held([P, PACK * QUARTER], BF16, "h_bf0"), held([P, PACK * QUARTER], BF16, "h_bf1")]
@@ -229,14 +227,14 @@ def tile_list_auction_lowrank_cross_kernel(
         for g in range(2):
             h_pass(accs[g], g, 1)
             relu(accs[g], h_bf[0], g)
-        quantize_h(h_bf[0], 0, QUARTER)
-        for g in range(2, 4):
-            h_pass(accs[g], g, 1)
-            relu(accs[g], h_bf[1], g - 2)
         x_acc = x_half(0, 0, 4)
+        quantize_h(h_bf[0], 0, QUARTER)
         for lo in (0, QUARTER):
             cols = slice(lo, lo + QUARTER)
             nc.vector.tensor_tensor(xw_sb[:, cols], x_acc[:, cols], wgo_sb[:, cols], MULT)
+        for g in range(2, 4):
+            h_pass(accs[g], g, 1)
+            relu(accs[g], h_bf[1], g - 2)
         finish_on_vector(0, 0, QUARTER, 7, xw_sb, y_sb)
         quantize_h(h_bf[1], QUARTER, HALF)
         scatter(0, 0, QUARTER, y_sb)
@@ -245,7 +243,7 @@ def tile_list_auction_lowrank_cross_kernel(
             relu(accs[g], h_bf[2], g - 4)
         xw_next = ring.tile([P, S], F32, name="xw_sb", align_bytes=64)
         y_next = ring.tile([P, S], F32, name="y_sb", align_bytes=64, bufs=3)
-        weighted_x(1, 0, 5, xw_next)
+        weighted_x(1, 0, 2, xw_next)
         for g in range(6, 8):
             acc = bank(g - 6, [P, PACK, GROUP])
             for a in range(PASSES):
@@ -256,7 +254,7 @@ def tile_list_auction_lowrank_cross_kernel(
         scatter(0, QUARTER, HALF, y_sb)
         finish_on_gpsimd(1, 0, HALF, 6, xw_next, y_next)
         scatter(1, 0, HALF, y_next)
-        for i, xw, y, x_bank, c_bank in ((0, xw_sb, y_sb, 2, 3), (1, xw_next, y_next, 4, 7)):
+        for i, xw, y, x_bank, c_bank in ((0, xw_sb, y_sb, 5, 3), (1, xw_next, y_next, 4, 7)):
             weighted_x(i, 1, x_bank, xw)
             finish_on_gpsimd(i, HALF, S, c_bank, xw, y)
             scatter(i, HALF, S, y)

@@ -25,8 +25,7 @@ TILES = N // P
 HALF = 512
 QUARTER = 256
 GROUP = 128
-CAST_SPLIT = 64
-ODD_SPLIT = 1023
+CAST_SPLIT = (32, 84)
 V_ROW, WX_ROW = 4, 8
 FIRST_TILES = 2
 
@@ -64,7 +63,8 @@ def tile_list_auction_lowrank_cross_kernel(
         ident = held([P, P], F32, "ident")
         cache = [held([P, T2], F32, f"cache{b}") for b in range(3)]
 
-        for plane in (tab_s, wu_s, wx_s):
+        nc.vector.memset(tab_s[:].bitcast(I32), 0)
+        for plane in (wu_s, wx_s):
             nc.gpsimd.memset(plane[:].bitcast(I32), 0)
         make_identity(nc, ident[:])
 
@@ -80,13 +80,13 @@ def tile_list_auction_lowrank_cross_kernel(
         def load_table(a):
             nc.sync.dma_start(tab_w[a][:], tab_words[a].rearrange("p t i -> p (t i)").bitcast(I32))
 
-        load_w1(0)
+        load_table(0)
         nc.sync.dma_start(gather_offs[:], offs)
         nc.sync.dma_start(
             b2_rows[:], b2.rearrange("(i p) -> i p", p=P).unsqueeze(0).broadcast_to([P // TILES, TILES, P])
         )
         load_scales(nc.sync, tab_s, V_ROW, tab_scales, PASSES)
-        load_table(0)
+        load_w1(0)
         load_scales(nc.sync, wu_s, 0, wu_scales, 1)
         load_w1(1)
         load_table(1)
@@ -102,10 +102,9 @@ def tile_list_auction_lowrank_cross_kernel(
         wgo_sb = held([P, S], F32, "ident")
         nc.sync.dma_start(wgo_sb[:, 0:HALF], wgo[:, 0:HALF])
 
-        nc.vector.memset(cache[0][:, 0:ODD_SPLIT], 0.0)
-        nc.vector.memset(cache[0][:, ODD_SPLIT:T2], 0.0)
-        for tile in cache[1:]:
+        for tile in cache[0:2]:
             nc.vector.memset(tile[:], 0.0)
+        nc.gpsimd.memset(cache[2][:], 0.0)
 
         def cast_views(a):
             dst = w1_bf[a][:].rearrange("p (t m j) -> p m t j", t=PACK, j=PACK)
@@ -114,30 +113,30 @@ def tile_list_auction_lowrank_cross_kernel(
         def quantize_w1(a):
             nc.vector.quantize_mx(out=w1_w[a][:].bitcast(FP8X4), scales=w1_s[a][:], in_=w1_bf[a][:])
 
-        def gather_words(a):
-            for lo, hi in ((0, QUARTER), (QUARTER, HALF), (HALF, S)):
+        def gather_words(a, cuts):
+            for lo, hi in cuts:
                 window = tab_w[a][:].bitcast(U32).indirect(gather_offs[:, lo // 16 : hi // 16])
                 nc.vector.tensor_copy(v_w[a][:, lo:hi], window)
 
         def cast_w1(a):
             dst, src = cast_views(a)
-            nc.vector.tensor_copy(dst[:, 0:CAST_SPLIT], src[:, 0:CAST_SPLIT])
-            nc.scalar.copy(dst[:, CAST_SPLIT:P], src[:, CAST_SPLIT:P])
+            nc.vector.tensor_copy(dst[:, 0 : CAST_SPLIT[a]], src[:, 0 : CAST_SPLIT[a]])
+            nc.scalar.copy(dst[:, CAST_SPLIT[a] : P], src[:, CAST_SPLIT[a] : P])
 
-        nc.scalar.copy(*cast_views(0))
-        bias = held([P, TILES], F32, "w1_raw0")
+        bias = held([P, TILES], F32, "bias")
         nc.scalar.activation(bias[:], b2_cols[:, 0:TILES], ACT.Copy, bias=1.0)
+        gather_words(0, [(0, S)])
         nc.vector.tensor_copy(v_s[:], tab_s[:].indirect(gather_offs[:]))
+        cast_w1(0)
         quantize_w1(0)
         wu_w = held([P, 2 * N], U8, "tab_s")
         nc.sync.dma_start(wu_w[:].bitcast(I32), wu_words[0].bitcast(I32))
         nc.sync.dma_start(wgo_sb[:, HALF:S], wgo[:, HALF:S])
-        gather_words(0)
-        wx_rest = held([P, PASSES, N - FIRST_TILES * P], I32, "tab_w0")
+        wx_rest = held([P, PASSES, N - FIRST_TILES * P], I32, "w1_raw0")
         nc.sync.dma_start(wx_rest[:], wx_src[:, :, FIRST_TILES * P : N])
         cast_w1(1)
         quantize_w1(1)
-        gather_words(1)
+        gather_words(1, [(0, QUARTER), (QUARTER, HALF), (HALF, S)])
 
         h_bf = [held([P, PACK * QUARTER], BF16, "h_bf0"), held([P, PACK * QUARTER], BF16, "h_bf1")]
         h_bf.append(held([P, PACK * HALF], BF16, "h_bf2"))
@@ -186,11 +185,11 @@ def tile_list_auction_lowrank_cross_kernel(
                 x_pass(acc[:], i, a, lo, lo + HALF, a == 0, a == PASSES - 1)
             return acc
 
-        def weighted_x(i, c, b, xw_sb):
+        def weighted_x(i, c, b, xw):
             acc = x_half(i, c, b)
             x_sb = ring.tile([P, HALF], F32, name="x_sb", align_bytes=64, bufs=3)
             nc.scalar.copy(x_sb[:], acc[:])
-            nc.gpsimd.tensor_tensor(xw_sb[:, c * HALF : (c + 1) * HALF], x_sb[:], wgo_sb[:, c * HALF : (c + 1) * HALF], MULT)
+            nc.gpsimd.tensor_tensor(xw, x_sb[:], wgo_sb[:, c * HALF : (c + 1) * HALF], MULT)
 
         def cross(i, lo, hi, b):
             acc = bank(b, [P, hi - lo])
@@ -209,20 +208,20 @@ def tile_list_auction_lowrank_cross_kernel(
             acc = cross(i, lo, hi, b)
             nc.vector.scalar_tensor_tensor(y_sb[:, lo:hi], acc[:], bias[:, i : i + 1], xw_sb[:, lo:hi], ADD, MULT)
 
-        def finish_on_gpsimd(i, lo, hi, b, xw_sb, y_sb):
+        def finish_on_gpsimd(i, lo, hi, b, xw, y_sb):
             c_sb = ring.tile([P, hi - lo], F32, name="c_sb", align_bytes=64, bufs=3)
             acc = cross(i, lo, hi, b)
             nc.scalar.activation(c_sb[:], acc[:], ACT.Identity, bias=bias[:, i : i + 1])
-            nc.gpsimd.tensor_tensor(y_sb[:, lo:hi], xw_sb[:, lo:hi], c_sb[:], MULT)
+            nc.gpsimd.tensor_tensor(y_sb[:, lo:hi], xw, c_sb[:], MULT)
 
         def scatter(i, lo, hi, y_sb):
             window = cache[i % 3][:].indirect(scatter_offs[:, lo // 16 : hi // 16])
             nc.vector.tensor_copy(window, y_sb[:, lo:hi])
 
-        xw_sb = ring.tile([P, S], F32, name="xw_sb", align_bytes=64)
+        xw_first = held([P, HALF], F32, "xw_first")
         y_sb = ring.tile([P, S], F32, name="y_sb", align_bytes=64, bufs=3)
-        accs = [bank(b, [P, PACK, GROUP]) for b in (0, 1, 2, 3, 5, 6)]
-        for g in range(6):
+        accs = [bank(b, [P, PACK, GROUP]) for b in range(4)]
+        for g in range(4):
             h_pass(accs[g], g, 0)
         for g in range(2):
             h_pass(accs[g], g, 1)
@@ -231,41 +230,50 @@ def tile_list_auction_lowrank_cross_kernel(
         quantize_h(h_bf[0], 0, QUARTER)
         for lo in (0, QUARTER):
             cols = slice(lo, lo + QUARTER)
-            nc.vector.tensor_tensor(xw_sb[:, cols], x_acc[:, cols], wgo_sb[:, cols], MULT)
+            nc.vector.tensor_tensor(xw_first[:, cols], x_acc[:, cols], wgo_sb[:, cols], MULT)
         for g in range(2, 4):
             h_pass(accs[g], g, 1)
             relu(accs[g], h_bf[1], g - 2)
-        finish_on_vector(0, 0, QUARTER, 7, xw_sb, y_sb)
+        finish_on_vector(0, 0, QUARTER, 7, xw_first, y_sb)
         quantize_h(h_bf[1], QUARTER, HALF)
         scatter(0, 0, QUARTER, y_sb)
-        for g in range(4, 6):
-            h_pass(accs[g], g, 1)
-            relu(accs[g], h_bf[2], g - 4)
-        xw_next = ring.tile([P, S], F32, name="xw_sb", align_bytes=64)
-        y_next = ring.tile([P, S], F32, name="y_sb", align_bytes=64, bufs=3)
-        weighted_x(1, 0, 2, xw_next)
-        for g in range(6, 8):
-            acc = bank(g - 6, [P, PACK, GROUP])
+        ys = [y_sb] + [ring.tile([P, S], F32, name="y_sb", align_bytes=64, bufs=3) for i in (1, 2)]
+        xws = [xw_first] + [held([P, HALF], F32, f"xw{i}") for i in (1, 2)]
+
+        def h_group(g, b):
+            acc = bank(b, [P, PACK, GROUP])
             for a in range(PASSES):
                 h_pass(acc, g, a)
             relu(acc, h_bf[2], g - 4)
-        finish_on_vector(0, QUARTER, HALF, 0, xw_sb, y_sb)
-        quantize_h(h_bf[2], HALF, S)
+
+        weighted_x(1, 0, 5, xws[1][:])
+        finish_on_vector(0, QUARTER, HALF, 4, xw_first, y_sb)
         scatter(0, QUARTER, HALF, y_sb)
-        finish_on_gpsimd(1, 0, HALF, 6, xw_next, y_next)
-        scatter(1, 0, HALF, y_next)
-        for i, xw, y, x_bank, c_bank in ((0, xw_sb, y_sb, 5, 3), (1, xw_next, y_next, 4, 7)):
-            weighted_x(i, 1, x_bank, xw)
-            finish_on_gpsimd(i, HALF, S, c_bank, xw, y)
-            scatter(i, HALF, S, y)
+        finish_on_gpsimd(1, 0, HALF, 6, xws[1][:], ys[1])
+        scatter(1, 0, HALF, ys[1])
+        h_group(4, 0)
+        weighted_x(2, 0, 6, xws[2][:])
+        finish_on_gpsimd(2, 0, HALF, 7, xws[2][:], ys[2])
+        for g, b in ((5, 1), (6, 3), (7, 5)):
+            h_group(g, b)
+        xw_late = held([P, HALF], F32, "xw_first")
+        weighted_x(0, 1, 0, xw_late[:])
+        quantize_h(h_bf[2], HALF, S)
+        scatter(2, 0, HALF, ys[2])
+        for i, name, x_bank, c_bank in ((0, None, None, 2), (1, "h_bf2", 1, 4), (2, "xw_first", 3, 6)):
+            if i > 0:
+                xw_late = held([P, HALF], F32, name)
+                weighted_x(i, 1, x_bank, xw_late[:])
+            finish_on_gpsimd(i, HALF, S, c_bank, xw_late[:], ys[i])
+            scatter(i, HALF, S, ys[i])
             nc.sync.dma_start(out[i * P : (i + 1) * P, :], cache[i][:])
 
-        for i in range(2, TILES):
+        for i in range(3, TILES):
             x_sb = ring.tile([P, S], F32, name="x_sb", align_bytes=64, bufs=3)
             c_sb = ring.tile([P, S], F32, name="c_sb", align_bytes=64, bufs=3)
-            xw_sb = ring.tile([P, S], F32, name="xw_sb", align_bytes=64)
+            xw_sb = held([P, S], F32, "xw_first")
             y_sb = ring.tile([P, S], F32, name="y_sb", align_bytes=64, bufs=3)
-            x_banks, c_banks = ((2, 4), (3, 7)) if i % 2 else ((0, 1), (5, 6))
+            x_banks, c_banks = ((2, 4), (5, 7)) if i % 2 else ((0, 1), (3, 6))
             for c in range(2):
                 nc.scalar.copy(x_sb[:, c * HALF : (c + 1) * HALF], x_half(i, c, x_banks[c])[:])
             nc.gpsimd.tensor_tensor(xw_sb[:], x_sb[:], wgo_sb[:], MULT)

@@ -25,7 +25,8 @@ TILES = N // P
 HALF = 512
 QUARTER = 256
 GROUP = 128
-CAST_SPLIT = (32, 84)
+ODD_SPLIT = 1023
+CAST_SPLIT = 64
 V_ROW, WX_ROW = 4, 8
 FIRST_TILES = 2
 
@@ -63,8 +64,7 @@ def tile_list_auction_lowrank_cross_kernel(
         ident = held([P, P], F32, "ident")
         cache = [held([P, T2], F32, f"cache{b}") for b in range(3)]
 
-        nc.vector.memset(tab_s[:].bitcast(I32), 0)
-        for plane in (wu_s, wx_s):
+        for plane in (tab_s, wu_s, wx_s):
             nc.gpsimd.memset(plane[:].bitcast(I32), 0)
         make_identity(nc, ident[:])
 
@@ -80,13 +80,13 @@ def tile_list_auction_lowrank_cross_kernel(
         def load_table(a):
             nc.sync.dma_start(tab_w[a][:], tab_words[a].rearrange("p t i -> p (t i)").bitcast(I32))
 
-        load_table(0)
+        load_w1(0)
         nc.sync.dma_start(gather_offs[:], offs)
         nc.sync.dma_start(
             b2_rows[:], b2.rearrange("(i p) -> i p", p=P).unsqueeze(0).broadcast_to([P // TILES, TILES, P])
         )
         load_scales(nc.sync, tab_s, V_ROW, tab_scales, PASSES)
-        load_w1(0)
+        load_table(0)
         load_scales(nc.sync, wu_s, 0, wu_scales, 1)
         load_w1(1)
         load_table(1)
@@ -102,9 +102,10 @@ def tile_list_auction_lowrank_cross_kernel(
         wgo_sb = held([P, S], F32, "ident")
         nc.sync.dma_start(wgo_sb[:, 0:HALF], wgo[:, 0:HALF])
 
-        for tile in cache[0:2]:
+        nc.vector.memset(cache[0][:, 0:ODD_SPLIT], 0.0)
+        nc.vector.memset(cache[0][:, ODD_SPLIT:T2], 0.0)
+        for tile in cache[1:]:
             nc.vector.memset(tile[:], 0.0)
-        nc.gpsimd.memset(cache[2][:], 0.0)
 
         def cast_views(a):
             dst = w1_bf[a][:].rearrange("p (t m j) -> p m t j", t=PACK, j=PACK)
@@ -113,30 +114,30 @@ def tile_list_auction_lowrank_cross_kernel(
         def quantize_w1(a):
             nc.vector.quantize_mx(out=w1_w[a][:].bitcast(FP8X4), scales=w1_s[a][:], in_=w1_bf[a][:])
 
-        def gather_words(a, cuts):
-            for lo, hi in cuts:
+        def gather_words(a):
+            for lo, hi in ((0, QUARTER), (QUARTER, HALF), (HALF, S)):
                 window = tab_w[a][:].bitcast(U32).indirect(gather_offs[:, lo // 16 : hi // 16])
                 nc.vector.tensor_copy(v_w[a][:, lo:hi], window)
 
         def cast_w1(a):
             dst, src = cast_views(a)
-            nc.vector.tensor_copy(dst[:, 0 : CAST_SPLIT[a]], src[:, 0 : CAST_SPLIT[a]])
-            nc.scalar.copy(dst[:, CAST_SPLIT[a] : P], src[:, CAST_SPLIT[a] : P])
+            nc.vector.tensor_copy(dst[:, 0:CAST_SPLIT], src[:, 0:CAST_SPLIT])
+            nc.scalar.copy(dst[:, CAST_SPLIT:P], src[:, CAST_SPLIT:P])
 
-        bias = held([P, TILES], F32, "bias")
+        nc.scalar.copy(*cast_views(0))
+        bias = held([P, TILES], F32, "w1_raw0")
         nc.scalar.activation(bias[:], b2_cols[:, 0:TILES], ACT.Copy, bias=1.0)
-        gather_words(0, [(0, S)])
         nc.vector.tensor_copy(v_s[:], tab_s[:].indirect(gather_offs[:]))
-        cast_w1(0)
         quantize_w1(0)
         wu_w = held([P, 2 * N], U8, "tab_s")
         nc.sync.dma_start(wu_w[:].bitcast(I32), wu_words[0].bitcast(I32))
         nc.sync.dma_start(wgo_sb[:, HALF:S], wgo[:, HALF:S])
-        wx_rest = held([P, PASSES, N - FIRST_TILES * P], I32, "w1_raw0")
+        gather_words(0)
+        wx_rest = held([P, PASSES, N - FIRST_TILES * P], I32, "tab_w0")
         nc.sync.dma_start(wx_rest[:], wx_src[:, :, FIRST_TILES * P : N])
         cast_w1(1)
         quantize_w1(1)
-        gather_words(1, [(0, QUARTER), (QUARTER, HALF), (HALF, S)])
+        gather_words(1)
 
         h_bf = [held([P, PACK * QUARTER], BF16, "h_bf0"), held([P, PACK * QUARTER], BF16, "h_bf1")]
         h_bf.append(held([P, PACK * HALF], BF16, "h_bf2"))
@@ -220,8 +221,8 @@ def tile_list_auction_lowrank_cross_kernel(
 
         xw_first = held([P, HALF], F32, "xw_first")
         y_sb = ring.tile([P, S], F32, name="y_sb", align_bytes=64, bufs=3)
-        accs = [bank(b, [P, PACK, GROUP]) for b in range(4)]
-        for g in range(4):
+        accs = [bank(b, [P, PACK, GROUP]) for b in (0, 1, 2, 3, 5, 6)]
+        for g in range(6):
             h_pass(accs[g], g, 0)
         for g in range(2):
             h_pass(accs[g], g, 1)
@@ -246,21 +247,24 @@ def tile_list_auction_lowrank_cross_kernel(
                 h_pass(acc, g, a)
             relu(acc, h_bf[2], g - 4)
 
-        weighted_x(1, 0, 5, xws[1][:])
-        finish_on_vector(0, QUARTER, HALF, 4, xw_first, y_sb)
+        weighted_x(1, 0, 0, xws[1][:])
+        finish_on_vector(0, QUARTER, HALF, 1, xw_first, y_sb)
         scatter(0, QUARTER, HALF, y_sb)
-        finish_on_gpsimd(1, 0, HALF, 6, xws[1][:], ys[1])
+        finish_on_gpsimd(1, 0, HALF, 2, xws[1][:], ys[1])
         scatter(1, 0, HALF, ys[1])
-        h_group(4, 0)
-        weighted_x(2, 0, 6, xws[2][:])
-        finish_on_gpsimd(2, 0, HALF, 7, xws[2][:], ys[2])
-        for g, b in ((5, 1), (6, 3), (7, 5)):
+        h_pass(accs[4], 4, 1)
+        relu(accs[4], h_bf[2], 0)
+        weighted_x(2, 0, 2, xws[2][:])
+        finish_on_gpsimd(2, 0, HALF, 3, xws[2][:], ys[2])
+        h_pass(accs[5], 5, 1)
+        relu(accs[5], h_bf[2], 1)
+        for g, b in ((6, 7), (7, 0)):
             h_group(g, b)
         xw_late = held([P, HALF], F32, "xw_first")
-        weighted_x(0, 1, 0, xw_late[:])
+        weighted_x(0, 1, 5, xw_late[:])
         quantize_h(h_bf[2], HALF, S)
         scatter(2, 0, HALF, ys[2])
-        for i, name, x_bank, c_bank in ((0, None, None, 2), (1, "h_bf2", 1, 4), (2, "xw_first", 3, 6)):
+        for i, name, x_bank, c_bank in ((0, None, None, 4), (1, "h_bf2", 6, 3), (2, "xw_first", 7, 2)):
             if i > 0:
                 xw_late = held([P, HALF], F32, name)
                 weighted_x(i, 1, x_bank, xw_late[:])
@@ -273,7 +277,7 @@ def tile_list_auction_lowrank_cross_kernel(
             c_sb = ring.tile([P, S], F32, name="c_sb", align_bytes=64, bufs=3)
             xw_sb = held([P, S], F32, "xw_first")
             y_sb = ring.tile([P, S], F32, name="y_sb", align_bytes=64, bufs=3)
-            x_banks, c_banks = ((2, 4), (5, 7)) if i % 2 else ((0, 1), (3, 6))
+            x_banks, c_banks = ((0, 5), (6, 7)) if i % 2 else ((4, 3), (2, 1))
             for c in range(2):
                 nc.scalar.copy(x_sb[:, c * HALF : (c + 1) * HALF], x_half(i, c, x_banks[c])[:])
             nc.gpsimd.tensor_tensor(xw_sb[:], x_sb[:], wgo_sb[:], MULT)

@@ -62,7 +62,7 @@ def tile_list_auction_lowrank_cross_kernel(
         h_s = held([P, S], U8, "h_s")
         b2_rows = held([P, P], F32, "b2_rows")
         ident = held([P, P], F32, "ident")
-        cache = [held([P, T2], F32, f"cache{b}") for b in range(3)]
+        cache = [held([P, T2], F32, f"cache{b}") for b in range(2)]
 
         for plane in (tab_s, wu_s, wx_s):
             nc.gpsimd.memset(plane[:].bitcast(I32), 0)
@@ -216,10 +216,10 @@ def tile_list_auction_lowrank_cross_kernel(
             nc.gpsimd.tensor_tensor(y_sb[:, lo:hi], xw, c_sb[:], MULT)
 
         def scatter(i, lo, hi, y_sb):
-            window = cache[i % 3][:].indirect(scatter_offs[:, lo // 16 : hi // 16])
+            window = cache[i % 2][:].indirect(scatter_offs[:, lo // 16 : hi // 16])
             nc.vector.tensor_copy(window, y_sb[:, lo:hi])
 
-        xw_first = held([P, HALF], F32, "xw_first")
+        xw_first = held([P, S], F32, "xw_first")
         y_sb = ring.tile([P, S], F32, name="y_sb", align_bytes=64, bufs=3)
         accs = [bank(b, [P, PACK, GROUP]) for b in (0, 1, 2, 3, 5, 6)]
         for g in range(6):
@@ -238,46 +238,29 @@ def tile_list_auction_lowrank_cross_kernel(
         finish_on_vector(0, 0, QUARTER, 7, xw_first, y_sb)
         quantize_h(h_bf[1], QUARTER, HALF)
         scatter(0, 0, QUARTER, y_sb)
-        ys = [y_sb] + [ring.tile([P, S], F32, name="y_sb", align_bytes=64, bufs=3) for i in (1, 2)]
-        xws = [xw_first] + [held([P, HALF], F32, f"xw{i}") for i in (1, 2)]
-
-        def h_group(g, b):
-            acc = bank(b, [P, PACK, GROUP])
+        for g in range(4, 6):
+            h_pass(accs[g], g, 1)
+            relu(accs[g], h_bf[2], g - 4)
+        for g in range(6, 8):
+            acc = bank(g - 6, [P, PACK, GROUP])
             for a in range(PASSES):
                 h_pass(acc, g, a)
             relu(acc, h_bf[2], g - 4)
-
-        weighted_x(1, 0, 0, xws[1][:])
-        finish_on_vector(0, QUARTER, HALF, 1, xw_first, y_sb)
-        scatter(0, QUARTER, HALF, y_sb)
-        finish_on_gpsimd(1, 0, HALF, 2, xws[1][:], ys[1])
-        scatter(1, 0, HALF, ys[1])
-        h_pass(accs[4], 4, 1)
-        relu(accs[4], h_bf[2], 0)
-        weighted_x(2, 0, 2, xws[2][:])
-        finish_on_gpsimd(2, 0, HALF, 3, xws[2][:], ys[2])
-        h_pass(accs[5], 5, 1)
-        relu(accs[5], h_bf[2], 1)
-        for g, b in ((6, 7), (7, 0)):
-            h_group(g, b)
-        xw_late = held([P, HALF], F32, "xw_first")
-        weighted_x(0, 1, 5, xw_late[:])
+        finish_on_vector(0, QUARTER, HALF, 0, xw_first, y_sb)
         quantize_h(h_bf[2], HALF, S)
-        scatter(2, 0, HALF, ys[2])
-        for i, name, x_bank, c_bank in ((0, None, None, 4), (1, "h_bf2", 6, 3), (2, "xw_first", 7, 2)):
-            if i > 0:
-                xw_late = held([P, HALF], F32, name)
-                weighted_x(i, 1, x_bank, xw_late[:])
-            finish_on_gpsimd(i, HALF, S, c_bank, xw_late[:], ys[i])
-            scatter(i, HALF, S, ys[i])
-            nc.sync.dma_start(out[i * P : (i + 1) * P, :], cache[i][:])
+        x_acc = x_half(0, 1, 4)
+        nc.vector.tensor_tensor(xw_first[:, HALF:S], x_acc[:], wgo_sb[:, HALF:S], MULT)
+        scatter(0, QUARTER, HALF, y_sb)
+        finish_on_vector(0, HALF, S, 7, xw_first, y_sb)
+        scatter(0, HALF, S, y_sb)
+        nc.sync.dma_start(out[0:P, :], cache[0][:])
 
-        for i in range(3, TILES):
+        for i in range(1, TILES):
             x_sb = ring.tile([P, S], F32, name="x_sb", align_bytes=64, bufs=3)
             c_sb = ring.tile([P, S], F32, name="c_sb", align_bytes=64, bufs=3)
-            xw_sb = held([P, S], F32, "xw_first")
+            xw_sb = ring.tile([P, S], F32, name="xw_sb", align_bytes=64)
             y_sb = ring.tile([P, S], F32, name="y_sb", align_bytes=64, bufs=3)
-            x_banks, c_banks = ((0, 5), (6, 7)) if i % 2 else ((4, 3), (2, 1))
+            x_banks, c_banks = ((6, 1), (2, 3)) if i % 2 else ((4, 5), (0, 7))
             for c in range(2):
                 nc.scalar.copy(x_sb[:, c * HALF : (c + 1) * HALF], x_half(i, c, x_banks[c])[:])
             nc.gpsimd.tensor_tensor(xw_sb[:], x_sb[:], wgo_sb[:], MULT)
@@ -286,4 +269,4 @@ def tile_list_auction_lowrank_cross_kernel(
                 nc.scalar.activation(c_sb[:, c * HALF : (c + 1) * HALF], acc[:], ACT.Identity, bias=bias[:, i : i + 1])
             nc.gpsimd.tensor_tensor(y_sb[:], xw_sb[:], c_sb[:], MULT)
             scatter(i, 0, S, y_sb)
-            nc.sync.dma_start(out[i * P : (i + 1) * P, :], cache[i % 3][:])
+            nc.sync.dma_start(out[i * P : (i + 1) * P, :], cache[i % 2][:])

@@ -26,7 +26,6 @@ HALF = 512
 QUARTER = 256
 GROUP = 128
 ODD_SPLIT = 1023
-CAST_SPLIT = 64
 V_ROW, WX_ROW = 4, 8
 FIRST_TILES = 2
 
@@ -51,27 +50,34 @@ def tile_list_auction_lowrank_cross_kernel(
         tab_s = held([P, T], U8, "tab_s")
         tab_w = [held([P, T], I32, f"tab_w{a}") for a in range(PASSES)]
         v_s = held([P, S], U8, "v_s")
-        v_w = [held([P, S], U32, f"v_w{a}") for a in range(PASSES)]
         w1_raw = [held([P, PACK, R], F32, f"w1_raw{a}") for a in range(PASSES)]
-        w1_bf = [held([P, PACK * R], BF16, f"w1_bf{a}") for a in range(PASSES)]
-        w1_w = [held([P, R], U32, f"w1_w{a}") for a in range(PASSES)]
         w1_s = [held([P, R], U8, f"w1_s{a}") for a in range(PASSES)]
         wx_s = held([P, N], U8, "wx_s")
         wu_s = held([P, N], U8, "wu_s")
+        wx_w = [held([P, PASSES, P], I32, f"wx_w{i}") for i in range(FIRST_TILES)]
+        wx_rest = held([P, PASSES, N - FIRST_TILES * P], I32, "wx_rest")
+        wu_first = held([P, 2 * FIRST_TILES * P], U8, "wu_first")
+        wu_rest = held([P, 2 * (N - FIRST_TILES * P)], U8, "wu_rest")
+        wgo_sb = held([P, S], F32, "wgo_sb")
         h_w = held([P, S], U32, "h_w")
         h_s = held([P, S], U8, "h_s")
         b2_rows = held([P, P], F32, "b2_rows")
+        bias = held([P, TILES], F32, "bias")
         ident = held([P, P], F32, "ident")
         cache = [held([P, T2], F32, f"cache{b}") for b in range(2)]
 
         for plane in (tab_s, wu_s, wx_s):
             nc.gpsimd.memset(plane[:].bitcast(I32), 0)
+        nc.gpsimd.memset(b2_rows[:], 0.0)
         make_identity(nc, ident[:])
+        nc.gpsimd.memset(cache[1][:], 0.0)
+        nc.vector.memset(cache[0][:, 0:ODD_SPLIT], 0.0)
+        nc.vector.memset(cache[0][:, ODD_SPLIT:T2], 0.0)
 
-        def load_scales(queue, plane, row, src, passes):
+        def load_scales(plane, row, src, passes, lo, hi):
             for q in range(4):
-                rows = plane[32 * q + row : 32 * q + row + 4 * passes, :]
-                queue.dma_start(rows.bitcast(I32), src[:, 4 * q : 4 * q + 4, :].bitcast(I32))
+                rows = plane[32 * q + row : 32 * q + row + 4 * passes, lo:hi]
+                nc.sync.dma_start(rows.bitcast(I32), src[:, 4 * q : 4 * q + 4, lo:hi].bitcast(I32))
 
         def load_w1(a):
             rows = w1[P * PACK * a : P * PACK * (a + 1), :]
@@ -80,64 +86,64 @@ def tile_list_auction_lowrank_cross_kernel(
         def load_table(a):
             nc.sync.dma_start(tab_w[a][:], tab_words[a].rearrange("p t i -> p (t i)").bitcast(I32))
 
+        wx_src = wx_words.rearrange("a p e i -> p a (e i)").bitcast(I32)
+        wu_src = wu_words[0].bitcast(I32)
+        first_words = FIRST_TILES * P // 2
+
         load_w1(0)
         nc.sync.dma_start(gather_offs[:], offs)
-        nc.sync.dma_start(
-            b2_rows[:], b2.rearrange("(i p) -> i p", p=P).unsqueeze(0).broadcast_to([P // TILES, TILES, P])
-        )
-        load_scales(nc.sync, tab_s, V_ROW, tab_scales, PASSES)
+        load_scales(tab_s, V_ROW, tab_scales, PASSES, 0, T)
         load_table(0)
-        load_scales(nc.sync, wu_s, 0, wu_scales, 1)
+        load_scales(wu_s, 0, wu_scales, 1, 0, N)
         load_w1(1)
+        load_scales(wx_s, WX_ROW, wx_scales, PASSES, 0, FIRST_TILES * P)
+        nc.sync.dma_start(b2_rows[0:TILES, :], b2.rearrange("(i p) -> i p", p=P))
         load_table(1)
+        nc.sync.dma_start(wx_w[0][:], wx_src[:, :, 0:P])
+        nc.sync.dma_start(wgo_sb[:, 0:HALF], wgo[:, 0:HALF])
+        nc.sync.dma_start(wgo_sb[:, HALF:S], wgo[:, HALF:S])
+        nc.sync.dma_start(wu_first[:].bitcast(I32), wu_src[:, 0:first_words])
         nc.sync.dma_start(scatter_offs[:], offs2)
-        load_scales(nc.gpsimd, wx_s, WX_ROW, wx_scales, PASSES)
+        nc.sync.dma_start(wx_w[1][:], wx_src[:, :, P : 2 * P])
+        load_scales(wx_s, WX_ROW, wx_scales, PASSES, FIRST_TILES * P, N)
+        nc.sync.dma_start(wx_rest[:], wx_src[:, :, FIRST_TILES * P : N])
+        nc.sync.dma_start(wu_rest[:].bitcast(I32), wu_src[:, first_words : N // 2])
 
+        v_w = []
+
+        def cast_w1(copy, a, u, name):
+            pair = held([P, 2 * R], BF16, name)
+            src = w1_raw[a][:].rearrange("p j (m t) -> p m t j", t=PACK)
+            copy(pair[:].rearrange("p (t m j) -> p m t j", t=2, j=PACK), src[:, :, 2 * u : 2 * u + 2, :])
+            return pair
+
+        def quantize_w1(a, u, pair):
+            cols = slice(2 * P * u, 2 * P * (u + 1))
+            nc.vector.quantize_mx(out=w1_w[a][:, cols].bitcast(FP8X4), scales=w1_s[a][:, cols], in_=pair[:])
+
+        def gather_words(a, lo, hi):
+            window = tab_w[a][:].bitcast(U32).indirect(gather_offs[:, lo // 16 : hi // 16])
+            nc.vector.tensor_copy(v_w[a][:, lo:hi], window)
+
+        low = cast_w1(nc.scalar.copy, 0, 0, "w1_low0")
+        high = cast_w1(nc.scalar.copy, 0, 1, "w1_high0")
+        nc.vector.tensor_copy(v_s[:], tab_s[:].indirect(gather_offs[:]))
+        w1_w = [held([P, R], U32, "tab_s"), held([P, R], U32, "w1_w1")]
+        quantize_w1(0, 0, low)
+        quantize_w1(0, 1, high)
+        v_w.append(held([P, S], U32, "w1_raw0"))
+        gather_words(0, 0, QUARTER)
+        gather_words(0, QUARTER, S)
+        high = cast_w1(nc.scalar.copy, 1, 1, "w1_high1")
+        low = cast_w1(nc.vector.tensor_copy, 1, 0, "tab_w0")
+        quantize_w1(1, 1, high)
+        quantize_w1(1, 0, low)
         b2_cols = bank(7, [P, P])
         nc.tensor.transpose(b2_cols[:], b2_rows[:], ident[:])
-
-        wx_src = wx_words.rearrange("a p e i -> p a (e i)").bitcast(I32)
-        wx_first = held([P, PASSES, FIRST_TILES * P], I32, "b2_rows")
-        nc.sync.dma_start(wx_first[:], wx_src[:, :, 0 : FIRST_TILES * P])
-        wgo_sb = held([P, S], F32, "ident")
-        nc.sync.dma_start(wgo_sb[:, 0:HALF], wgo[:, 0:HALF])
-
-        nc.vector.memset(cache[0][:, 0:ODD_SPLIT], 0.0)
-        nc.vector.memset(cache[0][:, ODD_SPLIT:T2], 0.0)
-        for tile in cache[1:]:
-            nc.vector.memset(tile[:], 0.0)
-
-        def cast_views(a):
-            dst = w1_bf[a][:].rearrange("p (t m j) -> p m t j", t=PACK, j=PACK)
-            return dst, w1_raw[a][:].rearrange("p j (m t) -> p m t j", t=PACK)
-
-        def quantize_w1(a):
-            nc.vector.quantize_mx(out=w1_w[a][:].bitcast(FP8X4), scales=w1_s[a][:], in_=w1_bf[a][:])
-
-        def gather_words(a):
-            for lo, hi in ((0, QUARTER), (QUARTER, HALF), (HALF, S)):
-                window = tab_w[a][:].bitcast(U32).indirect(gather_offs[:, lo // 16 : hi // 16])
-                nc.vector.tensor_copy(v_w[a][:, lo:hi], window)
-
-        def cast_w1(a):
-            dst, src = cast_views(a)
-            nc.vector.tensor_copy(dst[:, 0:CAST_SPLIT], src[:, 0:CAST_SPLIT])
-            nc.scalar.copy(dst[:, CAST_SPLIT:P], src[:, CAST_SPLIT:P])
-
-        nc.scalar.copy(*cast_views(0))
-        bias = held([P, TILES], F32, "w1_raw0")
         nc.scalar.activation(bias[:], b2_cols[:, 0:TILES], ACT.Copy, bias=1.0)
-        nc.vector.tensor_copy(v_s[:], tab_s[:].indirect(gather_offs[:]))
-        quantize_w1(0)
-        wu_w = held([P, 2 * N], U8, "tab_s")
-        nc.sync.dma_start(wu_w[:].bitcast(I32), wu_words[0].bitcast(I32))
-        nc.sync.dma_start(wgo_sb[:, HALF:S], wgo[:, HALF:S])
-        gather_words(0)
-        wx_rest = held([P, PASSES, N - FIRST_TILES * P], I32, "tab_w0")
-        nc.sync.dma_start(wx_rest[:], wx_src[:, :, FIRST_TILES * P : N])
-        cast_w1(1)
-        quantize_w1(1)
-        gather_words(1)
+        v_w.append(held([P, S], U32, "w1_raw1"))
+        for lo, hi in ((0, QUARTER), (QUARTER, HALF), (HALF, S)):
+            gather_words(1, lo, hi)
 
         h_bf = [held([P, PACK * QUARTER], BF16, "h_bf0"), held([P, PACK * QUARTER], BF16, "h_bf1")]
         h_bf.append(held([P, PACK * HALF], BF16, "h_bf2"))
@@ -165,38 +171,33 @@ def tile_list_auction_lowrank_cross_kernel(
         def quantize_h(src, lo, hi):
             nc.vector.quantize_mx(out=h_w[:, lo:hi].bitcast(FP8X4), scales=h_s[:, lo:hi], in_=src[:])
 
-        def x_pass(acc, i, a, lo, hi, start, stop):
-            wx_w = wx_first[:, a, i * P : (i + 1) * P] if i < FIRST_TILES else (
-                wx_rest[:, a, (i - FIRST_TILES) * P : (i - FIRST_TILES + 1) * P]
-            )
-            nc.tensor.matmul_mx(
-                out=acc,
-                lhsT=wx_w.bitcast(FP8X4),
-                lhsT_scale=wx_s[WX_ROW + 4 * a : P, i * P : (i + 1) * P],
-                rhs=v_w[a][:, lo:hi].bitcast(FP8X4),
-                rhs_scale=v_s[V_ROW + 4 * a : P, lo:hi],
-                start=start,
-                stop=stop,
-            )
-
-        def x_half(i, c, b):
-            acc = bank(b, [P, HALF])
-            lo = c * HALF
+        def project(i, lo, hi, b):
+            acc = bank(b, [P, hi - lo])
             for a in range(PASSES):
-                x_pass(acc[:], i, a, lo, lo + HALF, a == 0, a == PASSES - 1)
+                if i < FIRST_TILES:
+                    words = wx_w[i][:, a, :]
+                else:
+                    words = wx_rest[:, a, (i - FIRST_TILES) * P : (i - FIRST_TILES + 1) * P]
+                nc.tensor.matmul_mx(
+                    out=acc[:],
+                    lhsT=words.bitcast(FP8X4),
+                    lhsT_scale=wx_s[WX_ROW + 4 * a : P, i * P : (i + 1) * P],
+                    rhs=v_w[a][:, lo:hi].bitcast(FP8X4),
+                    rhs_scale=v_s[V_ROW + 4 * a : P, lo:hi],
+                    start=a == 0,
+                    stop=a == PASSES - 1,
+                )
             return acc
-
-        def weighted_x(i, c, b, xw):
-            acc = x_half(i, c, b)
-            x_sb = ring.tile([P, HALF], F32, name="x_sb", align_bytes=64, bufs=3)
-            nc.scalar.copy(x_sb[:], acc[:])
-            nc.gpsimd.tensor_tensor(xw, x_sb[:], wgo_sb[:, c * HALF : (c + 1) * HALF], MULT)
 
         def cross(i, lo, hi, b):
             acc = bank(b, [P, hi - lo])
+            if i < FIRST_TILES:
+                wu_w = wu_first[:, 2 * i * P : 2 * (i + 1) * P]
+            else:
+                wu_w = wu_rest[:, 2 * (i - FIRST_TILES) * P : 2 * (i - FIRST_TILES + 1) * P]
             nc.tensor.matmul_mx(
                 out=acc[:],
-                lhsT=wu_w[:, 2 * i * P : 2 * (i + 1) * P].bitcast(FP4X4),
+                lhsT=wu_w.bitcast(FP4X4),
                 lhsT_scale=wu_s[:, i * P : (i + 1) * P],
                 rhs=h_w[:, lo:hi].bitcast(FP8X4),
                 rhs_scale=h_s[:, lo:hi],
@@ -205,65 +206,68 @@ def tile_list_auction_lowrank_cross_kernel(
             )
             return acc
 
-        def finish_on_vector(i, lo, hi, b, xw_sb, y_sb):
-            acc = cross(i, lo, hi, b)
-            nc.vector.scalar_tensor_tensor(y_sb[:, lo:hi], acc[:], bias[:, i : i + 1], xw_sb[:, lo:hi], ADD, MULT)
-
-        def finish_on_gpsimd(i, lo, hi, b, xw, y_sb):
-            c_sb = ring.tile([P, hi - lo], F32, name="c_sb", align_bytes=64, bufs=3)
-            acc = cross(i, lo, hi, b)
-            nc.scalar.activation(c_sb[:], acc[:], ACT.Identity, bias=bias[:, i : i + 1])
-            nc.gpsimd.tensor_tensor(y_sb[:, lo:hi], xw, c_sb[:], MULT)
-
         def scatter(i, lo, hi, y_sb):
             window = cache[i % 2][:].indirect(scatter_offs[:, lo // 16 : hi // 16])
             nc.vector.tensor_copy(window, y_sb[:, lo:hi])
 
         xw_first = held([P, S], F32, "xw_first")
         y_sb = ring.tile([P, S], F32, name="y_sb", align_bytes=64, bufs=3)
+
+        def weigh_first(lo, hi, acc):
+            nc.vector.tensor_tensor(xw_first[:, lo:hi], acc[:], wgo_sb[:, lo:hi], MULT)
+
+        def finish_first(lo, hi, b):
+            acc = cross(0, lo, hi, b)
+            nc.vector.scalar_tensor_tensor(y_sb[:, lo:hi], acc[:], bias[:, 0:1], xw_first[:, lo:hi], ADD, MULT)
+
         accs = [bank(b, [P, PACK, GROUP]) for b in (0, 1, 2, 3, 5, 6)]
         for g in range(6):
             h_pass(accs[g], g, 0)
         for g in range(2):
             h_pass(accs[g], g, 1)
             relu(accs[g], h_bf[0], g)
-        x_acc = x_half(0, 0, 4)
+        weigh_first(0, HALF, project(0, 0, HALF, 4))
         quantize_h(h_bf[0], 0, QUARTER)
-        for lo in (0, QUARTER):
-            cols = slice(lo, lo + QUARTER)
-            nc.vector.tensor_tensor(xw_first[:, cols], x_acc[:, cols], wgo_sb[:, cols], MULT)
         for g in range(2, 4):
             h_pass(accs[g], g, 1)
             relu(accs[g], h_bf[1], g - 2)
-        finish_on_vector(0, 0, QUARTER, 7, xw_first, y_sb)
+        weigh_first(HALF, HALF + QUARTER, project(0, HALF, HALF + QUARTER, 7))
+        weigh_first(HALF + QUARTER, S, project(0, HALF + QUARTER, S, 0))
+        h_pass(accs[4], 4, 1)
+        relu(accs[4], h_bf[2], 0)
+        finish_first(0, QUARTER, 1)
         quantize_h(h_bf[1], QUARTER, HALF)
         scatter(0, 0, QUARTER, y_sb)
-        for g in range(4, 6):
-            h_pass(accs[g], g, 1)
-            relu(accs[g], h_bf[2], g - 4)
-        for g in range(6, 8):
-            acc = bank(g - 6, [P, PACK, GROUP])
+        h_pass(accs[5], 5, 1)
+        relu(accs[5], h_bf[2], 1)
+        for g, b in ((6, 4), (7, 2)):
+            acc = bank(b, [P, PACK, GROUP])
             for a in range(PASSES):
                 h_pass(acc, g, a)
             relu(acc, h_bf[2], g - 4)
-        finish_on_vector(0, QUARTER, HALF, 0, xw_first, y_sb)
+        finish_first(QUARTER, HALF, 4)
         quantize_h(h_bf[2], HALF, S)
-        x_acc = x_half(0, 1, 4)
-        nc.vector.tensor_tensor(xw_first[:, HALF:S], x_acc[:], wgo_sb[:, HALF:S], MULT)
         scatter(0, QUARTER, HALF, y_sb)
-        finish_on_vector(0, HALF, S, 7, xw_first, y_sb)
+        finish_first(HALF, S, 7)
         scatter(0, HALF, S, y_sb)
         nc.sync.dma_start(out[0:P, :], cache[0][:])
 
         for i in range(1, TILES):
             x_sb = ring.tile([P, S], F32, name="x_sb", align_bytes=64, bufs=3)
             c_sb = ring.tile([P, S], F32, name="c_sb", align_bytes=64, bufs=3)
-            xw_sb = ring.tile([P, S], F32, name="xw_sb", align_bytes=64)
+            if i == 1:
+                xw_sb = held([P, S], F32, "h_bf2")
+            else:
+                xw_sb = ring.tile([P, S], F32, name="xw_sb", align_bytes=64)
             y_sb = ring.tile([P, S], F32, name="y_sb", align_bytes=64, bufs=3)
-            x_banks, c_banks = ((6, 1), (2, 3)) if i % 2 else ((4, 5), (0, 7))
+            x_banks, c_banks = ((5, 6), (3, 0)) if i % 2 else ((1, 2), (4, 7))
             for c in range(2):
-                nc.scalar.copy(x_sb[:, c * HALF : (c + 1) * HALF], x_half(i, c, x_banks[c])[:])
-            nc.gpsimd.tensor_tensor(xw_sb[:], x_sb[:], wgo_sb[:], MULT)
+                cols = slice(c * HALF, (c + 1) * HALF)
+                nc.scalar.copy(x_sb[:, cols], project(i, c * HALF, (c + 1) * HALF, x_banks[c])[:])
+                if i == 1:
+                    nc.gpsimd.tensor_tensor(xw_sb[:, cols], x_sb[:, cols], wgo_sb[:, cols], MULT)
+            if i > 1:
+                nc.gpsimd.tensor_tensor(xw_sb[:], x_sb[:], wgo_sb[:], MULT)
             for c in range(2):
                 acc = cross(i, c * HALF, (c + 1) * HALF, c_banks[c])
                 nc.scalar.activation(c_sb[:, c * HALF : (c + 1) * HALF], acc[:], ACT.Identity, bias=bias[:, i : i + 1])

@@ -28,6 +28,9 @@ GROUP = 128
 ODD_SPLIT = 1023
 V_ROW, WX_ROW = 4, 8
 FIRST_TILES = 2
+CACHES = 3
+LEAD_COLUMNS = 512
+CAST_SPLIT = 104
 
 
 def tile_list_auction_lowrank_cross_kernel(
@@ -54,7 +57,7 @@ def tile_list_auction_lowrank_cross_kernel(
         w1_s = [held([P, R], U8, f"w1_s{a}") for a in range(PASSES)]
         wx_s = held([P, N], U8, "wx_s")
         wu_s = held([P, N], U8, "wu_s")
-        wx_w = [held([P, PASSES, P], I32, f"wx_w{i}") for i in range(FIRST_TILES)]
+        wx_first = held([P, PASSES, FIRST_TILES * P], I32, "wx_first")
         wx_rest = held([P, PASSES, N - FIRST_TILES * P], I32, "wx_rest")
         wu_first = held([P, 2 * FIRST_TILES * P], U8, "wu_first")
         wu_rest = held([P, 2 * (N - FIRST_TILES * P)], U8, "wu_rest")
@@ -64,84 +67,85 @@ def tile_list_auction_lowrank_cross_kernel(
         b2_rows = held([P, P], F32, "b2_rows")
         bias = held([P, TILES], F32, "bias")
         ident = held([P, P], F32, "ident")
-        cache = [held([P, T2], F32, f"cache{b}") for b in range(2)]
+        cache = [held([P, T2], F32, f"cache{b}") for b in range(CACHES)]
 
         for plane in (tab_s, wu_s, wx_s):
             nc.gpsimd.memset(plane[:].bitcast(I32), 0)
         nc.gpsimd.memset(b2_rows[:], 0.0)
-        make_identity(nc, ident[:])
-        nc.gpsimd.memset(cache[1][:], 0.0)
         nc.vector.memset(cache[0][:, 0:ODD_SPLIT], 0.0)
         nc.vector.memset(cache[0][:, ODD_SPLIT:T2], 0.0)
 
-        def load_scales(plane, row, src, passes, lo, hi):
+        def load_scales(queue, plane, row, src, passes, lo, hi):
             for q in range(4):
                 rows = plane[32 * q + row : 32 * q + row + 4 * passes, lo:hi]
-                nc.sync.dma_start(rows.bitcast(I32), src[:, 4 * q : 4 * q + 4, lo:hi].bitcast(I32))
+                queue.dma_start(rows.bitcast(I32), src[:, 4 * q : 4 * q + 4, lo:hi].bitcast(I32))
 
         def load_w1(a):
             rows = w1[P * PACK * a : P * PACK * (a + 1), :]
             nc.sync.dma_start(w1_raw[a][:], rows.rearrange("(p j) r -> p j r", j=PACK))
 
-        def load_table(a):
-            nc.sync.dma_start(tab_w[a][:], tab_words[a].rearrange("p t i -> p (t i)").bitcast(I32))
+        def load_table(a, lo, hi):
+            src = tab_words[a].rearrange("p t i -> p (t i)").bitcast(I32)
+            nc.sync.dma_start(tab_w[a][:, lo:hi], src[:, lo:hi])
 
         wx_src = wx_words.rearrange("a p e i -> p a (e i)").bitcast(I32)
         wu_src = wu_words[0].bitcast(I32)
         first_words = FIRST_TILES * P // 2
 
-        load_w1(0)
+        for tile in cache[1:]:
+            nc.gpsimd.memset(tile[:], 0.0)
+        make_identity(nc, ident[:])
+        load_scales(nc.gpsimd, wu_s, 0, wu_scales, 1, 0, N)
+        load_table(0, 0, LEAD_COLUMNS)
         nc.sync.dma_start(gather_offs[:], offs)
-        load_scales(tab_s, V_ROW, tab_scales, PASSES, 0, T)
-        load_table(0)
-        load_scales(wu_s, 0, wu_scales, 1, 0, N)
+        load_scales(nc.sync, tab_s, V_ROW, tab_scales, PASSES, 0, T)
+        load_w1(0)
+        load_table(0, LEAD_COLUMNS, T)
         load_w1(1)
-        load_scales(wx_s, WX_ROW, wx_scales, PASSES, 0, FIRST_TILES * P)
+        load_scales(nc.sync, wx_s, WX_ROW, wx_scales, PASSES, 0, FIRST_TILES * P)
         nc.sync.dma_start(b2_rows[0:TILES, :], b2.rearrange("(i p) -> i p", p=P))
-        load_table(1)
-        nc.sync.dma_start(wx_w[0][:], wx_src[:, :, 0:P])
+        load_table(1, 0, T)
+        nc.sync.dma_start(wx_first[:], wx_src[:, :, 0 : FIRST_TILES * P])
         nc.sync.dma_start(wgo_sb[:, 0:HALF], wgo[:, 0:HALF])
         nc.sync.dma_start(wgo_sb[:, HALF:S], wgo[:, HALF:S])
         nc.sync.dma_start(wu_first[:].bitcast(I32), wu_src[:, 0:first_words])
         nc.sync.dma_start(scatter_offs[:], offs2)
-        nc.sync.dma_start(wx_w[1][:], wx_src[:, :, P : 2 * P])
-        load_scales(wx_s, WX_ROW, wx_scales, PASSES, FIRST_TILES * P, N)
+        load_scales(nc.sync, wx_s, WX_ROW, wx_scales, PASSES, FIRST_TILES * P, N)
         nc.sync.dma_start(wx_rest[:], wx_src[:, :, FIRST_TILES * P : N])
         nc.sync.dma_start(wu_rest[:].bitcast(I32), wu_src[:, first_words : N // 2])
 
-        v_w = []
+        v_w = [held([P, S], U32, f"v_w{a}") for a in range(PASSES)]
+        w1_w = [held([P, R], U32, f"w1_w{a}") for a in range(PASSES)]
+        pairs = [[held([P, 2 * R], BF16, f"w1_pair{a}{u}") for u in range(2)] for a in range(PASSES)]
 
-        def cast_w1(copy, a, u, name):
-            pair = held([P, 2 * R], BF16, name)
+        def cast_w1(copy, a, u, lo, hi):
+            dst = pairs[a][u][:].rearrange("p (t m j) -> p m t j", t=2, j=PACK)
             src = w1_raw[a][:].rearrange("p j (m t) -> p m t j", t=PACK)
-            copy(pair[:].rearrange("p (t m j) -> p m t j", t=2, j=PACK), src[:, :, 2 * u : 2 * u + 2, :])
-            return pair
+            copy(dst[:, lo:hi], src[:, lo:hi, 2 * u : 2 * u + 2, :])
 
-        def quantize_w1(a, u, pair):
+        def quantize_w1(a, u):
             cols = slice(2 * P * u, 2 * P * (u + 1))
-            nc.vector.quantize_mx(out=w1_w[a][:, cols].bitcast(FP8X4), scales=w1_s[a][:, cols], in_=pair[:])
+            nc.vector.quantize_mx(out=w1_w[a][:, cols].bitcast(FP8X4), scales=w1_s[a][:, cols], in_=pairs[a][u][:])
 
         def gather_words(a, lo, hi):
             window = tab_w[a][:].bitcast(U32).indirect(gather_offs[:, lo // 16 : hi // 16])
             nc.vector.tensor_copy(v_w[a][:, lo:hi], window)
 
-        low = cast_w1(nc.scalar.copy, 0, 0, "w1_low0")
-        high = cast_w1(nc.scalar.copy, 0, 1, "w1_high0")
         nc.vector.tensor_copy(v_s[:], tab_s[:].indirect(gather_offs[:]))
-        w1_w = [held([P, R], U32, "tab_s"), held([P, R], U32, "w1_w1")]
-        quantize_w1(0, 0, low)
-        quantize_w1(0, 1, high)
-        v_w.append(held([P, S], U32, "w1_raw0"))
+        cast_w1(nc.scalar.copy, 0, 1, 0, P)
+        cast_w1(nc.vector.tensor_copy, 0, 0, 0, P)
+        quantize_w1(0, 0)
+        quantize_w1(0, 1)
         gather_words(0, 0, QUARTER)
         gather_words(0, QUARTER, S)
-        high = cast_w1(nc.scalar.copy, 1, 1, "w1_high1")
-        low = cast_w1(nc.vector.tensor_copy, 1, 0, "tab_w0")
-        quantize_w1(1, 1, high)
-        quantize_w1(1, 0, low)
+        cast_w1(nc.scalar.copy, 1, 1, 0, P)
+        cast_w1(nc.scalar.copy, 1, 0, CAST_SPLIT, P)
+        cast_w1(nc.vector.tensor_copy, 1, 0, 0, CAST_SPLIT)
+        quantize_w1(1, 1)
+        quantize_w1(1, 0)
         b2_cols = bank(7, [P, P])
         nc.tensor.transpose(b2_cols[:], b2_rows[:], ident[:])
         nc.scalar.activation(bias[:], b2_cols[:, 0:TILES], ACT.Copy, bias=1.0)
-        v_w.append(held([P, S], U32, "w1_raw1"))
         for lo, hi in ((0, QUARTER), (QUARTER, HALF), (HALF, S)):
             gather_words(1, lo, hi)
 
@@ -175,7 +179,7 @@ def tile_list_auction_lowrank_cross_kernel(
             acc = bank(b, [P, hi - lo])
             for a in range(PASSES):
                 if i < FIRST_TILES:
-                    words = wx_w[i][:, a, :]
+                    words = wx_first[:, a, i * P : (i + 1) * P]
                 else:
                     words = wx_rest[:, a, (i - FIRST_TILES) * P : (i - FIRST_TILES + 1) * P]
                 nc.tensor.matmul_mx(
@@ -207,7 +211,7 @@ def tile_list_auction_lowrank_cross_kernel(
             return acc
 
         def scatter(i, lo, hi, y_sb):
-            window = cache[i % 2][:].indirect(scatter_offs[:, lo // 16 : hi // 16])
+            window = cache[i % CACHES][:].indirect(scatter_offs[:, lo // 16 : hi // 16])
             nc.vector.tensor_copy(window, y_sb[:, lo:hi])
 
         xw_first = held([P, S], F32, "xw_first")
@@ -232,11 +236,31 @@ def tile_list_auction_lowrank_cross_kernel(
             h_pass(accs[g], g, 1)
             relu(accs[g], h_bf[1], g - 2)
         weigh_first(HALF, HALF + QUARTER, project(0, HALF, HALF + QUARTER, 7))
-        weigh_first(HALF + QUARTER, S, project(0, HALF + QUARTER, S, 0))
-        h_pass(accs[4], 4, 1)
-        relu(accs[4], h_bf[2], 0)
+
+        def copy_x(i, lo, hi, b):
+            x_sb = ring.tile([P, hi - lo], F32, name="x_sb", align_bytes=64, bufs=3)
+            nc.scalar.copy(x_sb[:], project(i, lo, hi, b)[:])
+            return x_sb
+
+        def copy_c(i, lo, hi, b):
+            c_sb = ring.tile([P, hi - lo], F32, name="c_sb", align_bytes=64, bufs=3)
+            nc.scalar.activation(c_sb[:], cross(i, lo, hi, b)[:], ACT.Identity, bias=bias[:, i : i + 1])
+            return c_sb
+
+        def multiply(dst, left, right):
+            nc.gpsimd.tensor_tensor(dst, left, right, MULT)
+
+        def store(i):
+            nc.sync.dma_start(out[i * P : (i + 1) * P, :], cache[i % CACHES][:])
+
+        x_low = copy_x(1, 0, HALF, 0)
         finish_first(0, QUARTER, 1)
         quantize_h(h_bf[1], QUARTER, HALF)
+        xw_low = held([P, HALF], F32, "h_bf1")
+        multiply(xw_low[:], x_low[:], wgo_sb[:, 0:HALF])
+        h_pass(accs[4], 4, 1)
+        relu(accs[4], h_bf[2], 0)
+        weigh_first(HALF + QUARTER, S, project(0, HALF + QUARTER, S, 3))
         scatter(0, 0, QUARTER, y_sb)
         h_pass(accs[5], 5, 1)
         relu(accs[5], h_bf[2], 1)
@@ -248,29 +272,31 @@ def tile_list_auction_lowrank_cross_kernel(
         finish_first(QUARTER, HALF, 4)
         quantize_h(h_bf[2], HALF, S)
         scatter(0, QUARTER, HALF, y_sb)
-        finish_first(HALF, S, 7)
-        scatter(0, HALF, S, y_sb)
-        nc.sync.dma_start(out[0:P, :], cache[0][:])
 
-        for i in range(1, TILES):
-            x_sb = ring.tile([P, S], F32, name="x_sb", align_bytes=64, bufs=3)
-            c_sb = ring.tile([P, S], F32, name="c_sb", align_bytes=64, bufs=3)
-            if i == 1:
-                xw_sb = held([P, S], F32, "h_bf2")
-            else:
-                xw_sb = ring.tile([P, S], F32, name="xw_sb", align_bytes=64)
+        y_second = held([P, S], F32, "h_bf2")
+        multiply(y_second[:, 0:HALF], xw_low[:], copy_c(1, 0, HALF, 0)[:])
+        scatter(1, 0, HALF, y_second)
+        xw_high = held([P, HALF], F32, "xw_high")
+        multiply(xw_high[:], copy_x(1, HALF, S, 2)[:], wgo_sb[:, HALF:S])
+        multiply(y_sb[:, HALF:S], xw_first[:, HALF:S], copy_c(0, HALF, S, 5)[:])
+        scatter(0, HALF, S, y_sb)
+        store(0)
+        multiply(y_second[:, HALF:S], xw_high[:], copy_c(1, HALF, S, 7)[:])
+        scatter(1, HALF, S, y_second)
+        store(1)
+
+        for i in range(FIRST_TILES, TILES):
+            x_sb = ring.tile([P, S], F32, name="x_whole", align_bytes=64, bufs=3)
+            c_sb = ring.tile([P, S], F32, name="c_whole", align_bytes=64, bufs=3)
+            xw_sb = ring.tile([P, S], F32, name="xw_sb", align_bytes=64)
             y_sb = ring.tile([P, S], F32, name="y_sb", align_bytes=64, bufs=3)
-            x_banks, c_banks = ((5, 6), (3, 0)) if i % 2 else ((1, 2), (4, 7))
+            x_banks, c_banks = ((2, 6), (5, 7)) if i % 2 else ((0, 1), (3, 4))
             for c in range(2):
-                cols = slice(c * HALF, (c + 1) * HALF)
-                nc.scalar.copy(x_sb[:, cols], project(i, c * HALF, (c + 1) * HALF, x_banks[c])[:])
-                if i == 1:
-                    nc.gpsimd.tensor_tensor(xw_sb[:, cols], x_sb[:, cols], wgo_sb[:, cols], MULT)
-            if i > 1:
-                nc.gpsimd.tensor_tensor(xw_sb[:], x_sb[:], wgo_sb[:], MULT)
+                nc.scalar.copy(x_sb[:, c * HALF : (c + 1) * HALF], project(i, c * HALF, (c + 1) * HALF, x_banks[c])[:])
+            multiply(xw_sb[:], x_sb[:], wgo_sb[:])
             for c in range(2):
                 acc = cross(i, c * HALF, (c + 1) * HALF, c_banks[c])
                 nc.scalar.activation(c_sb[:, c * HALF : (c + 1) * HALF], acc[:], ACT.Identity, bias=bias[:, i : i + 1])
-            nc.gpsimd.tensor_tensor(y_sb[:], xw_sb[:], c_sb[:], MULT)
+            multiply(y_sb[:], xw_sb[:], c_sb[:])
             scatter(i, 0, S, y_sb)
-            nc.sync.dma_start(out[i * P : (i + 1) * P, :], cache[i % 2][:])
+            store(i)

@@ -28,6 +28,7 @@ GROUP = 128
 ODD_SPLIT = 1023
 V_ROW, WX_ROW = 4, 8
 FIRST_TILES = 2
+HALVED_TILES = 3
 CACHES = 3
 LEAD_COLUMNS = 512
 CAST_SPLIT = 104
@@ -58,9 +59,10 @@ def tile_list_auction_lowrank_cross_kernel(
         wx_s = held([P, N], U8, "wx_s")
         wu_s = held([P, N], U8, "wu_s")
         wx_first = held([P, PASSES, FIRST_TILES * P], I32, "wx_first")
-        wx_rest = held([P, PASSES, N - FIRST_TILES * P], I32, "wx_rest")
-        wu_first = held([P, 2 * FIRST_TILES * P], U8, "wu_first")
-        wu_rest = held([P, 2 * (N - FIRST_TILES * P)], U8, "wu_rest")
+        wx_rest = held([P, PASSES, N - HALVED_TILES * P], I32, "wx_rest")
+        wx_third = held([P, PASSES, P], I32, "wx_third")
+        wu_first = held([P, 2 * HALVED_TILES * P], U8, "wu_first")
+        wu_rest = held([P, 2 * (N - HALVED_TILES * P)], U8, "wu_rest")
         wgo_sb = held([P, S], F32, "wgo_sb")
         h_w = held([P, S], U32, "h_w")
         h_s = held([P, S], U8, "h_s")
@@ -90,7 +92,7 @@ def tile_list_auction_lowrank_cross_kernel(
 
         wx_src = wx_words.rearrange("a p e i -> p a (e i)").bitcast(I32)
         wu_src = wu_words[0].bitcast(I32)
-        first_words = FIRST_TILES * P // 2
+        first_words = HALVED_TILES * P // 2
 
         for tile in cache[1:]:
             nc.gpsimd.memset(tile[:], 0.0)
@@ -102,7 +104,7 @@ def tile_list_auction_lowrank_cross_kernel(
         load_w1(0)
         load_table(0, LEAD_COLUMNS, T)
         load_w1(1)
-        load_scales(nc.sync, wx_s, WX_ROW, wx_scales, PASSES, 0, FIRST_TILES * P)
+        load_scales(nc.sync, wx_s, WX_ROW, wx_scales, PASSES, 0, HALVED_TILES * P)
         nc.sync.dma_start(b2_rows[0:TILES, :], b2.rearrange("(i p) -> i p", p=P))
         load_table(1, 0, T)
         nc.sync.dma_start(wx_first[:], wx_src[:, :, 0 : FIRST_TILES * P])
@@ -110,8 +112,9 @@ def tile_list_auction_lowrank_cross_kernel(
         nc.sync.dma_start(wgo_sb[:, HALF:S], wgo[:, HALF:S])
         nc.sync.dma_start(wu_first[:].bitcast(I32), wu_src[:, 0:first_words])
         nc.sync.dma_start(scatter_offs[:], offs2)
-        load_scales(nc.sync, wx_s, WX_ROW, wx_scales, PASSES, FIRST_TILES * P, N)
-        nc.sync.dma_start(wx_rest[:], wx_src[:, :, FIRST_TILES * P : N])
+        nc.sync.dma_start(wx_third[:], wx_src[:, :, FIRST_TILES * P : HALVED_TILES * P])
+        load_scales(nc.sync, wx_s, WX_ROW, wx_scales, PASSES, HALVED_TILES * P, N)
+        nc.sync.dma_start(wx_rest[:], wx_src[:, :, HALVED_TILES * P : N])
         nc.sync.dma_start(wu_rest[:].bitcast(I32), wu_src[:, first_words : N // 2])
 
         v_w = [held([P, S], U32, f"v_w{a}") for a in range(PASSES)]
@@ -180,8 +183,10 @@ def tile_list_auction_lowrank_cross_kernel(
             for a in range(PASSES):
                 if i < FIRST_TILES:
                     words = wx_first[:, a, i * P : (i + 1) * P]
+                elif i < HALVED_TILES:
+                    words = wx_third[:, a, :]
                 else:
-                    words = wx_rest[:, a, (i - FIRST_TILES) * P : (i - FIRST_TILES + 1) * P]
+                    words = wx_rest[:, a, (i - HALVED_TILES) * P : (i - HALVED_TILES + 1) * P]
                 nc.tensor.matmul_mx(
                     out=acc[:],
                     lhsT=words.bitcast(FP8X4),
@@ -195,10 +200,10 @@ def tile_list_auction_lowrank_cross_kernel(
 
         def cross(i, lo, hi, b):
             acc = bank(b, [P, hi - lo])
-            if i < FIRST_TILES:
+            if i < HALVED_TILES:
                 wu_w = wu_first[:, 2 * i * P : 2 * (i + 1) * P]
             else:
-                wu_w = wu_rest[:, 2 * (i - FIRST_TILES) * P : 2 * (i - FIRST_TILES + 1) * P]
+                wu_w = wu_rest[:, 2 * (i - HALVED_TILES) * P : 2 * (i - HALVED_TILES + 1) * P]
             nc.tensor.matmul_mx(
                 out=acc[:],
                 lhsT=wu_w.bitcast(FP4X4),
@@ -276,21 +281,31 @@ def tile_list_auction_lowrank_cross_kernel(
         y_second = held([P, S], F32, "h_bf2")
         multiply(y_second[:, 0:HALF], xw_low[:], copy_c(1, 0, HALF, 0)[:])
         scatter(1, 0, HALF, y_second)
-        xw_high = held([P, HALF], F32, "xw_high")
-        multiply(xw_high[:], copy_x(1, HALF, S, 2)[:], wgo_sb[:, HALF:S])
+
+        def weigh_half(i, lo, hi, b):
+            xw_half = ring.tile([P, HALF], F32, name="xw_half", align_bytes=64, bufs=3)
+            multiply(xw_half[:], copy_x(i, lo, hi, b)[:], wgo_sb[:, lo:hi])
+            return xw_half
+
+        y_third = held([P, S], F32, "y_third")
+        xw_third = weigh_half(2, 0, HALF, 2)
         multiply(y_sb[:, HALF:S], xw_first[:, HALF:S], copy_c(0, HALF, S, 5)[:])
         scatter(0, HALF, S, y_sb)
         store(0)
-        multiply(y_second[:, HALF:S], xw_high[:], copy_c(1, HALF, S, 7)[:])
-        scatter(1, HALF, S, y_second)
-        store(1)
+        multiply(y_third[:, 0:HALF], xw_third[:], copy_c(2, 0, HALF, 7)[:])
+        scatter(2, 0, HALF, y_third)
+        xw_high = [weigh_half(1, HALF, S, 0), weigh_half(2, HALF, S, 2)]
+        for i, y_tile, b in ((1, y_second, 5), (2, y_third, 7)):
+            multiply(y_tile[:, HALF:S], xw_high[i - 1][:], copy_c(i, HALF, S, b)[:])
+            scatter(i, HALF, S, y_tile)
+            store(i)
 
-        for i in range(FIRST_TILES, TILES):
+        for i in range(HALVED_TILES, TILES):
             x_sb = ring.tile([P, S], F32, name="x_whole", align_bytes=64, bufs=3)
             c_sb = ring.tile([P, S], F32, name="c_whole", align_bytes=64, bufs=3)
             xw_sb = ring.tile([P, S], F32, name="xw_sb", align_bytes=64)
             y_sb = ring.tile([P, S], F32, name="y_sb", align_bytes=64, bufs=3)
-            x_banks, c_banks = ((2, 6), (5, 7)) if i % 2 else ((0, 1), (3, 4))
+            x_banks, c_banks = ((0, 2), (5, 7)) if i % 2 else ((1, 6), (3, 4))
             for c in range(2):
                 nc.scalar.copy(x_sb[:, c * HALF : (c + 1) * HALF], project(i, c * HALF, (c + 1) * HALF, x_banks[c])[:])
             multiply(xw_sb[:], x_sb[:], wgo_sb[:])

@@ -139,8 +139,8 @@ def tile_list_auction_lowrank_cross_kernel(
         cast_w1(nc.vector.tensor_copy, 0, 0, 0, P)
         quantize_w1(0, 0)
         quantize_w1(0, 1)
-        gather_words(0, 0, QUARTER)
-        gather_words(0, QUARTER, S)
+        for lo, hi in ((0, QUARTER), (QUARTER, HALF), (HALF, S)):
+            gather_words(0, lo, hi)
         cast_w1(nc.scalar.copy, 1, 1, 0, P)
         cast_w1(nc.scalar.copy, 1, 0, CAST_SPLIT, P)
         cast_w1(nc.vector.tensor_copy, 1, 0, 0, CAST_SPLIT)
@@ -149,7 +149,7 @@ def tile_list_auction_lowrank_cross_kernel(
         b2_cols = bank(7, [P, P])
         nc.tensor.transpose(b2_cols[:], b2_rows[:], ident[:])
         nc.scalar.activation(bias[:], b2_cols[:, 0:TILES], ACT.Copy, bias=1.0)
-        for lo, hi in ((0, QUARTER), (QUARTER, HALF), (HALF, S)):
+        for lo, hi in ((0, GROUP), (GROUP, QUARTER), (QUARTER, HALF), (HALF, S)):
             gather_words(1, lo, hi)
 
         h_bf = [held([P, PACK * QUARTER], BF16, "h_bf0"), held([P, PACK * QUARTER], BF16, "h_bf1")]
@@ -219,11 +219,11 @@ def tile_list_auction_lowrank_cross_kernel(
             window = cache[i % CACHES][:].indirect(scatter_offs[:, lo // 16 : hi // 16])
             nc.vector.tensor_copy(window, y_sb[:, lo:hi])
 
-        xw_first = held([P, S], F32, "xw_first")
+        xw_first = held([P, HALF], F32, "xw_first")
         y_sb = ring.tile([P, S], F32, name="y_sb", align_bytes=64, bufs=3)
 
         def weigh_first(lo, hi, acc):
-            nc.vector.tensor_tensor(xw_first[:, lo:hi], acc[:], wgo_sb[:, lo:hi], MULT)
+            nc.vector.tensor_tensor(xw_first[:, lo:hi], acc, wgo_sb[:, lo:hi], MULT)
 
         def finish_first(lo, hi, b):
             acc = cross(0, lo, hi, b)
@@ -232,15 +232,13 @@ def tile_list_auction_lowrank_cross_kernel(
         accs = [bank(b, [P, PACK, GROUP]) for b in (0, 1, 2, 3, 5, 6)]
         for g in range(6):
             h_pass(accs[g], g, 0)
-        for g in range(2):
+        for g in range(4):
             h_pass(accs[g], g, 1)
-            relu(accs[g], h_bf[0], g)
-        weigh_first(0, HALF, project(0, 0, HALF, 4))
+            relu(accs[g], h_bf[g // 2], g % 2)
         quantize_h(h_bf[0], 0, QUARTER)
-        for g in range(2, 4):
-            h_pass(accs[g], g, 1)
-            relu(accs[g], h_bf[1], g - 2)
-        weigh_first(HALF, HALF + QUARTER, project(0, HALF, HALF + QUARTER, 7))
+        x_first = project(0, 0, HALF, 4)
+        for lo in (0, QUARTER):
+            weigh_first(lo, lo + QUARTER, x_first[:, lo : lo + QUARTER])
 
         def copy_x(i, lo, hi, b):
             x_sb = ring.tile([P, hi - lo], F32, name="x_sb", align_bytes=64, bufs=3)
@@ -258,14 +256,13 @@ def tile_list_auction_lowrank_cross_kernel(
         def store(i):
             nc.sync.dma_start(out[i * P : (i + 1) * P, :], cache[i % CACHES][:])
 
+        finish_first(0, QUARTER, 7)
         x_low = copy_x(1, 0, HALF, 0)
-        finish_first(0, QUARTER, 1)
         quantize_h(h_bf[1], QUARTER, HALF)
         xw_low = held([P, HALF], F32, "h_bf1")
         multiply(xw_low[:], x_low[:], wgo_sb[:, 0:HALF])
         h_pass(accs[4], 4, 1)
         relu(accs[4], h_bf[2], 0)
-        weigh_first(HALF + QUARTER, S, project(0, HALF + QUARTER, S, 3))
         scatter(0, 0, QUARTER, y_sb)
         h_pass(accs[5], 5, 1)
         relu(accs[5], h_bf[2], 1)
@@ -288,13 +285,14 @@ def tile_list_auction_lowrank_cross_kernel(
             return xw_half
 
         y_third = held([P, S], F32, "y_third")
-        xw_third = weigh_half(2, 0, HALF, 2)
-        multiply(y_sb[:, HALF:S], xw_first[:, HALF:S], copy_c(0, HALF, S, 5)[:])
+        xw_last = weigh_half(0, HALF, S, 2)
+        multiply(y_sb[:, HALF:S], xw_last[:], copy_c(0, HALF, S, 5)[:])
         scatter(0, HALF, S, y_sb)
         store(0)
+        xw_third = weigh_half(2, 0, HALF, 5)
         multiply(y_third[:, 0:HALF], xw_third[:], copy_c(2, 0, HALF, 7)[:])
         scatter(2, 0, HALF, y_third)
-        xw_high = [weigh_half(1, HALF, S, 0), weigh_half(2, HALF, S, 2)]
+        xw_high = [weigh_half(1, HALF, S, 2), weigh_half(2, HALF, S, 0)]
         for i, y_tile, b in ((1, y_second, 5), (2, y_third, 7)):
             multiply(y_tile[:, HALF:S], xw_high[i - 1][:], copy_c(i, HALF, S, b)[:])
             scatter(i, HALF, S, y_tile)

@@ -152,8 +152,7 @@ def tile_list_auction_lowrank_cross_kernel(
         for lo, hi in ((0, GROUP), (GROUP, QUARTER), (QUARTER, HALF), (HALF, S)):
             gather_words(1, lo, hi)
 
-        h_bf = [held([P, PACK * QUARTER], BF16, "h_bf0"), held([P, PACK * QUARTER], BF16, "h_bf1")]
-        h_bf.append(held([P, PACK * HALF], BF16, "h_bf2"))
+        h_bf = [held([P, PACK * QUARTER], BF16, f"h_bf{q}") for q in range(S // QUARTER)]
 
         def h_pass(acc, g, a):
             lo, hi = g * GROUP, (g + 1) * GROUP
@@ -266,16 +265,17 @@ def tile_list_auction_lowrank_cross_kernel(
         scatter(0, 0, QUARTER, y_sb)
         h_pass(accs[5], 5, 1)
         relu(accs[5], h_bf[2], 1)
+        quantize_h(h_bf[2], HALF, HALF + QUARTER)
         for g, b in ((6, 4), (7, 2)):
             acc = bank(b, [P, PACK, GROUP])
             for a in range(PASSES):
                 h_pass(acc, g, a)
-            relu(acc, h_bf[2], g - 4)
+            relu(acc, h_bf[3], g - 6)
         finish_first(QUARTER, HALF, 4)
-        quantize_h(h_bf[2], HALF, S)
+        quantize_h(h_bf[3], HALF + QUARTER, S)
         scatter(0, QUARTER, HALF, y_sb)
 
-        y_second = held([P, S], F32, "h_bf2")
+        y_second = held([P, S], F32, "h_bf3")
         multiply(y_second[:, 0:HALF], xw_low[:], copy_c(1, 0, HALF, 0)[:])
         scatter(1, 0, HALF, y_second)
 

@@ -279,37 +279,16 @@ def tile_list_auction_lowrank_cross_kernel(
         multiply(y_second[:, 0:HALF], xw_low[:], copy_c(1, 0, HALF, 0)[:])
         scatter(1, 0, HALF, y_second)
 
-        def weigh_half(i, lo, hi, b):
-            xw_half = ring.tile([P, HALF], F32, name="xw_half", align_bytes=64, bufs=3)
-            multiply(xw_half[:], copy_x(i, lo, hi, b)[:], wgo_sb[:, lo:hi])
-            return xw_half
-
-        y_third = held([P, S], F32, "y_third")
-        xw_last = weigh_half(0, HALF, S, 2)
-        multiply(y_sb[:, HALF:S], xw_last[:], copy_c(0, HALF, S, 5)[:])
-        scatter(0, HALF, S, y_sb)
-        store(0)
-        xw_third = weigh_half(2, 0, HALF, 5)
-        multiply(y_third[:, 0:HALF], xw_third[:], copy_c(2, 0, HALF, 7)[:])
-        scatter(2, 0, HALF, y_third)
-        xw_high = [weigh_half(1, HALF, S, 2), weigh_half(2, HALF, S, 0)]
-        for i, y_tile, b in ((1, y_second, 5), (2, y_third, 7)):
-            multiply(y_tile[:, HALF:S], xw_high[i - 1][:], copy_c(i, HALF, S, b)[:])
-            scatter(i, HALF, S, y_tile)
-            store(i)
-
-        for i in range(HALVED_TILES, TILES):
-            x_sb = ring.tile([P, S], F32, name="x_whole", align_bytes=64, bufs=3)
-            c_sb = ring.tile([P, S], F32, name="c_whole", align_bytes=64, bufs=3)
-            xw_sb = ring.tile([P, S], F32, name="xw_sb", align_bytes=64)
-            y_sb = ring.tile([P, S], F32, name="y_sb", align_bytes=64, bufs=3)
-            x_banks, c_banks = ((0, 2), (5, 7)) if i % 2 else ((1, 6), (3, 4))
-            for c in range(2):
-                nc.scalar.copy(x_sb[:, c * HALF : (c + 1) * HALF], project(i, c * HALF, (c + 1) * HALF, x_banks[c])[:])
-            multiply(xw_sb[:], x_sb[:], wgo_sb[:])
-            for c in range(2):
-                acc = cross(i, c * HALF, (c + 1) * HALF, c_banks[c])
-                nc.scalar.activation(c_sb[:, c * HALF : (c + 1) * HALF], acc[:], ACT.Identity, bias=bias[:, i : i + 1])
-            multiply(y_sb[:], xw_sb[:], c_sb[:])
-            scatter(i, 0, S, y_sb)
-            store(i)
+        y_tiles = {0: y_sb, 1: y_second}
+        halves = [(0, 1)] + [pair for i in range(1, TILES) for pair in ((i + 1, 0), (i, 1)) if pair[0] < TILES]
+        for n, (i, c) in enumerate(halves):
+            lo, hi = c * HALF, (c + 1) * HALF
+            x_bank, c_bank = ((2, 5), (5, 2))[n % 2]
+            if i not in y_tiles:
+                y_tiles[i] = ring.tile([P, S], F32, name="y_sb", align_bytes=64, bufs=3)
+            xw_half = ring.tile([P, HALF], F32, name="xw_half", align_bytes=64)
+            multiply(xw_half[:], copy_x(i, lo, hi, x_bank)[:], wgo_sb[:, lo:hi])
+            multiply(y_tiles[i][:, lo:hi], xw_half[:], copy_c(i, lo, hi, c_bank)[:])
+            scatter(i, lo, hi, y_tiles[i])
+            if c == 1:
+                store(i)

@@ -30,6 +30,7 @@ V_ROW, WX_ROW = 4, 8
 FIRST_TILES = 2
 HALVED_TILES = 3
 CACHES = 3
+VECTOR_ZEROES = 640
 LEAD_COLUMNS = 512
 CAST_SPLIT = 104
 
@@ -76,6 +77,8 @@ def tile_list_auction_lowrank_cross_kernel(
         nc.gpsimd.memset(b2_rows[:], 0.0)
         nc.vector.memset(cache[0][:, 0:ODD_SPLIT], 0.0)
         nc.vector.memset(cache[0][:, ODD_SPLIT:T2], 0.0)
+        nc.vector.memset(cache[2][:, 0 : VECTOR_ZEROES - 1], 0.0)
+        nc.vector.memset(cache[2][:, VECTOR_ZEROES - 1 : VECTOR_ZEROES], 0.0)
 
         def load_scales(queue, plane, row, src, passes, lo, hi):
             for q in range(4):
@@ -94,8 +97,8 @@ def tile_list_auction_lowrank_cross_kernel(
         wu_src = wu_words[0].bitcast(I32)
         first_words = HALVED_TILES * P // 2
 
-        for tile in cache[1:]:
-            nc.gpsimd.memset(tile[:], 0.0)
+        nc.gpsimd.memset(cache[1][:], 0.0)
+        nc.gpsimd.memset(cache[2][:, VECTOR_ZEROES:T2], 0.0)
         make_identity(nc, ident[:])
         load_scales(nc.gpsimd, wu_s, 0, wu_scales, 1, 0, N)
         load_table(0, 0, LEAD_COLUMNS)
@@ -228,14 +231,14 @@ def tile_list_auction_lowrank_cross_kernel(
             acc = cross(0, lo, hi, b)
             nc.vector.scalar_tensor_tensor(y_sb[:, lo:hi], acc[:], bias[:, 0:1], xw_first[:, lo:hi], ADD, MULT)
 
-        accs = [bank(b, [P, PACK, GROUP]) for b in (0, 1, 2, 3, 5, 6)]
-        for g in range(6):
+        accs = [bank(b, [P, PACK, GROUP]) for b in (0, 1, 2, 3, 5, 6, 4)]
+        for g in range(7):
             h_pass(accs[g], g, 0)
         for g in range(4):
             h_pass(accs[g], g, 1)
             relu(accs[g], h_bf[g // 2], g % 2)
         quantize_h(h_bf[0], 0, QUARTER)
-        x_first = project(0, 0, HALF, 4)
+        x_first = project(0, 0, HALF, 7)
         for lo in (0, QUARTER):
             weigh_first(lo, lo + QUARTER, x_first[:, lo : lo + QUARTER])
 
@@ -255,7 +258,7 @@ def tile_list_auction_lowrank_cross_kernel(
         def store(i):
             nc.sync.dma_start(out[i * P : (i + 1) * P, :], cache[i % CACHES][:])
 
-        finish_first(0, QUARTER, 7)
+        finish_first(0, QUARTER, 1)
         x_low = copy_x(1, 0, HALF, 0)
         quantize_h(h_bf[1], QUARTER, HALF)
         xw_low = held([P, HALF], F32, "h_bf1")
@@ -266,11 +269,12 @@ def tile_list_auction_lowrank_cross_kernel(
         h_pass(accs[5], 5, 1)
         relu(accs[5], h_bf[2], 1)
         quantize_h(h_bf[2], HALF, HALF + QUARTER)
-        for g, b in ((6, 4), (7, 2)):
-            acc = bank(b, [P, PACK, GROUP])
-            for a in range(PASSES):
-                h_pass(acc, g, a)
-            relu(acc, h_bf[3], g - 6)
+        h_pass(accs[6], 6, 1)
+        relu(accs[6], h_bf[3], 0)
+        acc = bank(2, [P, PACK, GROUP])
+        for a in range(PASSES):
+            h_pass(acc, 7, a)
+        relu(acc, h_bf[3], 1)
         finish_first(QUARTER, HALF, 4)
         quantize_h(h_bf[3], HALF + QUARTER, S)
         scatter(0, QUARTER, HALF, y_sb)

@@ -266,31 +266,33 @@ def tile_list_auction_lowrank_cross_kernel(
         h_pass(accs[4], 4, 1)
         relu(accs[4], h_bf[2], 0)
         scatter(0, 0, QUARTER, y_sb)
+        finish_first(QUARTER, HALF, 5)
         h_pass(accs[5], 5, 1)
         relu(accs[5], h_bf[2], 1)
         quantize_h(h_bf[2], HALF, HALF + QUARTER)
+        scatter(0, QUARTER, HALF, y_sb)
         h_pass(accs[6], 6, 1)
         relu(accs[6], h_bf[3], 0)
+        y_second = held([P, S], F32, "h_bf2")
+        multiply(y_second[:, 0:HALF], xw_low[:], copy_c(1, 0, HALF, 0)[:])
         acc = bank(2, [P, PACK, GROUP])
         for a in range(PASSES):
             h_pass(acc, 7, a)
         relu(acc, h_bf[3], 1)
-        finish_first(QUARTER, HALF, 4)
         quantize_h(h_bf[3], HALF + QUARTER, S)
-        scatter(0, QUARTER, HALF, y_sb)
-
-        y_second = held([P, S], F32, "h_bf3")
-        multiply(y_second[:, 0:HALF], xw_low[:], copy_c(1, 0, HALF, 0)[:])
         scatter(1, 0, HALF, y_second)
 
         y_tiles = {0: y_sb, 1: y_second}
         halves = [(0, 1)] + [pair for i in range(1, TILES) for pair in ((i + 1, 0), (i, 1)) if pair[0] < TILES]
         for n, (i, c) in enumerate(halves):
             lo, hi = c * HALF, (c + 1) * HALF
-            x_bank, c_bank = ((2, 5), (5, 2))[n % 2]
+            x_bank, c_bank = (6, 2) if n == 1 else ((2, 5), (5, 2))[n % 2]
             if i not in y_tiles:
                 y_tiles[i] = ring.tile([P, S], F32, name="y_sb", align_bytes=64, bufs=3)
-            xw_half = ring.tile([P, HALF], F32, name="xw_half", align_bytes=64)
+            if n < 2:
+                xw_half = held([P, HALF], F32, "h_bf3")
+            else:
+                xw_half = ring.tile([P, HALF], F32, name="xw_half", align_bytes=64)
             multiply(xw_half[:], copy_x(i, lo, hi, x_bank)[:], wgo_sb[:, lo:hi])
             multiply(y_tiles[i][:, lo:hi], xw_half[:], copy_c(i, lo, hi, c_bank)[:])
             scatter(i, lo, hi, y_tiles[i])

@@ -26,7 +26,7 @@ HALF = 512
 QUARTER = 256
 GROUP = 128
 ODD_SPLIT = 1023
-V_ROW, WX_ROW = 4, 8
+V_ROW, WX_ROW = 0, 4
 FIRST_TILES = 2
 HALVED_TILES = 3
 CACHES = 3
@@ -81,7 +81,7 @@ def tile_list_auction_lowrank_cross_kernel(
         nc.vector.memset(cache[2][:, VECTOR_ZEROES - 1 : VECTOR_ZEROES], 0.0)
 
         def load_scales(queue, plane, row, src, passes, lo, hi):
-            for q in range(4):
+            for q in (2, 3, 0, 1):
                 rows = plane[32 * q + row : 32 * q + row + 4 * passes, lo:hi]
                 queue.dma_start(rows.bitcast(I32), src[:, 4 * q : 4 * q + 4, lo:hi].bitcast(I32))
 

from contextlib import ExitStack

import concourse.mybir as mybir
from concourse.masks import make_identity

K, R, N, T, S, T2 = 1024, 512, 1024, 2048, 1024, 2048
FLOPS = 2 * S * (K * N + K * R + R * N)

F32 = mybir.dt.float32
BF16 = mybir.dt.bfloat16
I32 = mybir.dt.int32
U32 = mybir.dt.uint32
U16 = mybir.dt.uint16
U8 = mybir.dt.uint8
FP8X4 = mybir.dt.float8_e4m3fn_x4
FP4X4 = mybir.dt.float4_e2m1fn_x4
MULT = mybir.AluOpType.mult
ADD = mybir.AluOpType.add
ACT = mybir.ActivationFunctionType

P = 128
PACK = 4
PASSES = K // (P * PACK)
TILES = N // P
HALF = 512
QUARTER = 256
GROUP = 128
ODD_SPLIT = 1023
V_ROW, WX_ROW = 0, 4
FIRST_TILES = 2
HALVED_TILES = 3
CACHES = 3
VECTOR_ZEROES = 640
LEAD_COLUMNS = 512
CAST_SPLIT = 104


def tile_list_auction_lowrank_cross_kernel(
    tc, tab_words, tab_scales, offs, w1, wx_words, wx_scales, wu_words, wu_scales, b2, wgo, offs2, out
):
    nc = tc.nc
    with ExitStack() as ctx:
        keep = ctx.enter_context(tc.tile_pool(name="keep", bufs=1))
        ring = ctx.enter_context(tc.tile_pool(name="ring", bufs=2))
        psum = ctx.enter_context(tc.psum_pool(name="psum", bufs=1))

        def bank(b, shape):
            return psum.tile(shape, F32, name=f"bank{b}")

        def held(shape, dtype, name):
            return keep.tile(shape, dtype, name=name, align_bytes=64)

        gather_offs = keep.tile([P, S // 16], U16, name="gather_offs")
        scatter_offs = keep.tile([P, S // 16], U16, name="scatter_offs")
        tab_s = held([P, T], U8, "tab_s")
        tab_w = [held([P, T], I32, f"tab_w{a}") for a in range(PASSES)]
        v_s = held([P, S], U8, "v_s")
        w1_raw = [held([P, PACK, R], F32, f"w1_raw{a}") for a in range(PASSES)]
        w1_s = [held([P, R], U8, f"w1_s{a}") for a in range(PASSES)]
        wx_s = held([P, N], U8, "wx_s")
        wu_s = held([P, N], U8, "wu_s")
        wx_first = held([P, PASSES, FIRST_TILES * P], I32, "wx_first")
        wx_rest = held([P, PASSES, N - HALVED_TILES * P], I32, "wx_rest")
        wx_third = held([P, PASSES, P], I32, "wx_third")
        wu_first = held([P, 2 * HALVED_TILES * P], U8, "wu_first")
        wu_rest = held([P, 2 * (N - HALVED_TILES * P)], U8, "wu_rest")
        wgo_sb = held([P, S], F32, "wgo_sb")
        h_w = held([P, S], U32, "h_w")
        h_s = held([P, S], U8, "h_s")
        b2_rows = held([P, P], F32, "b2_rows")
        bias = held([P, TILES], F32, "bias")
        ident = held([P, P], F32, "ident")
        cache = [held([P, T2], F32, f"cache{b}") for b in range(CACHES)]

        for plane in (tab_s, wu_s, wx_s):
            nc.gpsimd.memset(plane[:].bitcast(I32), 0)
        nc.gpsimd.memset(b2_rows[:], 0.0)
        nc.vector.memset(cache[0][:, 0:ODD_SPLIT], 0.0)
        nc.vector.memset(cache[0][:, ODD_SPLIT:T2], 0.0)
        nc.vector.memset(cache[2][:, 0 : VECTOR_ZEROES - 1], 0.0)
        nc.vector.memset(cache[2][:, VECTOR_ZEROES - 1 : VECTOR_ZEROES], 0.0)

        def load_scales(queue, plane, row, src, passes, lo, hi):
            for q in (2, 3, 0, 1):
                rows = plane[32 * q + row : 32 * q + row + 4 * passes, lo:hi]
                queue.dma_start(rows.bitcast(I32), src[:, 4 * q : 4 * q + 4, lo:hi].bitcast(I32))

        def load_w1(a):
            rows = w1[P * PACK * a : P * PACK * (a + 1), :]
            nc.sync.dma_start(w1_raw[a][:], rows.rearrange("(p j) r -> p j r", j=PACK))

        def load_table(a, lo, hi):
            src = tab_words[a].rearrange("p t i -> p (t i)").bitcast(I32)
            nc.sync.dma_start(tab_w[a][:, lo:hi], src[:, lo:hi])

        wx_src = wx_words.rearrange("a p e i -> p a (e i)").bitcast(I32)
        wu_src = wu_words[0].bitcast(I32)
        first_words = HALVED_TILES * P // 2

        nc.gpsimd.memset(cache[1][:], 0.0)
        nc.gpsimd.memset(cache[2][:, VECTOR_ZEROES:T2], 0.0)
        make_identity(nc, ident[:])
        load_scales(nc.gpsimd, wu_s, 0, wu_scales, 1, 0, N)
        load_table(0, 0, LEAD_COLUMNS)
        nc.sync.dma_start(gather_offs[:], offs)
        load_scales(nc.sync, tab_s, V_ROW, tab_scales, PASSES, 0, T)
        load_w1(0)
        load_table(0, LEAD_COLUMNS, T)
        load_w1(1)
        load_scales(nc.sync, wx_s, WX_ROW, wx_scales, PASSES, 0, HALVED_TILES * P)
        nc.sync.dma_start(b2_rows[0:TILES, :], b2.rearrange("(i p) -> i p", p=P))
        load_table(1, 0, T)
        nc.sync.dma_start(wx_first[:], wx_src[:, :, 0 : FIRST_TILES * P])
        nc.sync.dma_start(wgo_sb[:, 0:HALF], wgo[:, 0:HALF])
        nc.sync.dma_start(wgo_sb[:, HALF:S], wgo[:, HALF:S])
        nc.sync.dma_start(wu_first[:].bitcast(I32), wu_src[:, 0:first_words])
        nc.sync.dma_start(scatter_offs[:], offs2)
        nc.sync.dma_start(wx_third[:], wx_src[:, :, FIRST_TILES * P : HALVED_TILES * P])
        load_scales(nc.sync, wx_s, WX_ROW, wx_scales, PASSES, HALVED_TILES * P, N)
        nc.sync.dma_start(wx_rest[:], wx_src[:, :, HALVED_TILES * P : N])
        nc.sync.dma_start(wu_rest[:].bitcast(I32), wu_src[:, first_words : N // 2])

        v_w = [held([P, S], U32, f"v_w{a}") for a in range(PASSES)]
        w1_w = [held([P, R], U32, f"w1_w{a}") for a in range(PASSES)]
        pairs = [[held([P, 2 * R], BF16, f"w1_pair{a}{u}") for u in range(2)] for a in range(PASSES)]

        def cast_w1(copy, a, u, lo, hi):
            dst = pairs[a][u][:].rearrange("p (t m j) -> p m t j", t=2, j=PACK)
            src = w1_raw[a][:].rearrange("p j (m t) -> p m t j", t=PACK)
            copy(dst[:, lo:hi], src[:, lo:hi, 2 * u : 2 * u + 2, :])

        def quantize_w1(a, u):
            cols = slice(2 * P * u, 2 * P * (u + 1))
            nc.vector.quantize_mx(out=w1_w[a][:, cols].bitcast(FP8X4), scales=w1_s[a][:, cols], in_=pairs[a][u][:])

        def gather_words(a, lo, hi):
            window = tab_w[a][:].bitcast(U32).indirect(gather_offs[:, lo // 16 : hi // 16])
            nc.vector.tensor_copy(v_w[a][:, lo:hi], window)

        nc.vector.tensor_copy(v_s[:], tab_s[:].indirect(gather_offs[:]))
        cast_w1(nc.scalar.copy, 0, 1, 0, P)
        cast_w1(nc.vector.tensor_copy, 0, 0, 0, P)
        quantize_w1(0, 0)
        quantize_w1(0, 1)
        for lo, hi in ((0, QUARTER), (QUARTER, HALF), (HALF, S)):
            gather_words(0, lo, hi)
        cast_w1(nc.scalar.copy, 1, 1, 0, P)
        cast_w1(nc.scalar.copy, 1, 0, CAST_SPLIT, P)
        cast_w1(nc.vector.tensor_copy, 1, 0, 0, CAST_SPLIT)
        quantize_w1(1, 1)
        quantize_w1(1, 0)
        b2_cols = bank(7, [P, P])
        nc.tensor.transpose(b2_cols[:], b2_rows[:], ident[:])
        nc.scalar.activation(bias[:], b2_cols[:, 0:TILES], ACT.Copy, bias=1.0)
        for lo, hi in ((0, GROUP), (GROUP, QUARTER), (QUARTER, HALF), (HALF, S)):
            gather_words(1, lo, hi)

        h_bf = [held([P, PACK * QUARTER], BF16, f"h_bf{q}") for q in range(S // QUARTER)]

        def h_pass(acc, g, a):
            lo, hi = g * GROUP, (g + 1) * GROUP
            for t in range(PACK):
                nc.tensor.matmul_mx(
                    out=acc[:, t, :],
                    lhsT=w1_w[a][:, t * P : (t + 1) * P].bitcast(FP8X4),
                    lhsT_scale=w1_s[a][:, t * P : (t + 1) * P],
                    rhs=v_w[a][:, lo:hi].bitcast(FP8X4),
                    rhs_scale=v_s[V_ROW + 4 * a : P, lo:hi],
                    start=(a == 0 and t == 0),
                    stop=(a == PASSES - 1 and t == PACK - 1),
                )

        def relu(acc, dst, k):
            nc.scalar.activation(
                dst[:, PACK * k * GROUP : PACK * (k + 1) * GROUP].rearrange("p (j t) -> p j t", t=PACK),
                acc[:].rearrange("p t j -> p j t"),
                ACT.Relu,
            )

        def quantize_h(src, lo, hi):
            nc.vector.quantize_mx(out=h_w[:, lo:hi].bitcast(FP8X4), scales=h_s[:, lo:hi], in_=src[:])

        def project(i, lo, hi, b):
            acc = bank(b, [P, hi - lo])
            for a in range(PASSES):
                if i < FIRST_TILES:
                    words = wx_first[:, a, i * P : (i + 1) * P]
                elif i < HALVED_TILES:
                    words = wx_third[:, a, :]
                else:
                    words = wx_rest[:, a, (i - HALVED_TILES) * P : (i - HALVED_TILES + 1) * P]
                nc.tensor.matmul_mx(
                    out=acc[:],
                    lhsT=words.bitcast(FP8X4),
                    lhsT_scale=wx_s[WX_ROW + 4 * a : P, i * P : (i + 1) * P],
                    rhs=v_w[a][:, lo:hi].bitcast(FP8X4),
                    rhs_scale=v_s[V_ROW + 4 * a : P, lo:hi],
                    start=a == 0,
                    stop=a == PASSES - 1,
                )
            return acc

        def cross(i, lo, hi, b):
            acc = bank(b, [P, hi - lo])
            if i < HALVED_TILES:
                wu_w = wu_first[:, 2 * i * P : 2 * (i + 1) * P]
            else:
                wu_w = wu_rest[:, 2 * (i - HALVED_TILES) * P : 2 * (i - HALVED_TILES + 1) * P]
            nc.tensor.matmul_mx(
                out=acc[:],
                lhsT=wu_w.bitcast(FP4X4),
                lhsT_scale=wu_s[:, i * P : (i + 1) * P],
                rhs=h_w[:, lo:hi].bitcast(FP8X4),
                rhs_scale=h_s[:, lo:hi],
                start=True,
                stop=True,
            )
            return acc

        def scatter(i, lo, hi, y_sb):
            window = cache[i % CACHES][:].indirect(scatter_offs[:, lo // 16 : hi // 16])
            nc.vector.tensor_copy(window, y_sb[:, lo:hi])

        xw_first = held([P, HALF], F32, "xw_first")
        y_sb = ring.tile([P, S], F32, name="y_sb", align_bytes=64, bufs=3)

        def weigh_first(lo, hi, acc):
            nc.vector.tensor_tensor(xw_first[:, lo:hi], acc, wgo_sb[:, lo:hi], MULT)

        def finish_first(lo, hi, b):
            acc = cross(0, lo, hi, b)
            nc.vector.scalar_tensor_tensor(y_sb[:, lo:hi], acc[:], bias[:, 0:1], xw_first[:, lo:hi], ADD, MULT)

        accs = [bank(b, [P, PACK, GROUP]) for b in (0, 1, 2, 3, 5, 6, 4)]
        for g in range(7):
            h_pass(accs[g], g, 0)
        for g in range(4):
            h_pass(accs[g], g, 1)
            relu(accs[g], h_bf[g // 2], g % 2)
        quantize_h(h_bf[0], 0, QUARTER)
        x_first = project(0, 0, HALF, 7)
        for lo in (0, QUARTER):
            weigh_first(lo, lo + QUARTER, x_first[:, lo : lo + QUARTER])

        def copy_x(i, lo, hi, b):
            x_sb = ring.tile([P, hi - lo], F32, name="x_sb", align_bytes=64, bufs=3)
            nc.scalar.copy(x_sb[:], project(i, lo, hi, b)[:])
            return x_sb

        def copy_c(i, lo, hi, b):
            c_sb = ring.tile([P, hi - lo], F32, name="c_sb", align_bytes=64, bufs=3)
            nc.scalar.activation(c_sb[:], cross(i, lo, hi, b)[:], ACT.Identity, bias=bias[:, i : i + 1])
            return c_sb

        def multiply(dst, left, right):
            nc.gpsimd.tensor_tensor(dst, left, right, MULT)

        def store(i):
            nc.sync.dma_start(out[i * P : (i + 1) * P, :], cache[i % CACHES][:])

        finish_first(0, QUARTER, 1)
        x_low = copy_x(1, 0, HALF, 0)
        quantize_h(h_bf[1], QUARTER, HALF)
        xw_low = held([P, HALF], F32, "h_bf1")
        multiply(xw_low[:], x_low[:], wgo_sb[:, 0:HALF])
        h_pass(accs[4], 4, 1)
        relu(accs[4], h_bf[2], 0)
        scatter(0, 0, QUARTER, y_sb)
        finish_first(QUARTER, HALF, 5)
        h_pass(accs[5], 5, 1)
        relu(accs[5], h_bf[2], 1)
        quantize_h(h_bf[2], HALF, HALF + QUARTER)
        scatter(0, QUARTER, HALF, y_sb)
        h_pass(accs[6], 6, 1)
        relu(accs[6], h_bf[3], 0)
        y_second = held([P, S], F32, "h_bf2")
        multiply(y_second[:, 0:HALF], xw_low[:], copy_c(1, 0, HALF, 0)[:])
        acc = bank(2, [P, PACK, GROUP])
        for a in range(PASSES):
            h_pass(acc, 7, a)
        relu(acc, h_bf[3], 1)
        quantize_h(h_bf[3], HALF + QUARTER, S)
        scatter(1, 0, HALF, y_second)

        y_tiles = {0: y_sb, 1: y_second}
        halves = [(0, 1)] + [pair for i in range(1, TILES) for pair in ((i + 1, 0), (i, 1)) if pair[0] < TILES]
        for n, (i, c) in enumerate(halves):
            lo, hi = c * HALF, (c + 1) * HALF
            x_bank, c_bank = (6, 2) if n == 1 else ((2, 5), (5, 2))[n % 2]
            if i not in y_tiles:
                y_tiles[i] = ring.tile([P, S], F32, name="y_sb", align_bytes=64, bufs=3)
            if n < 2:
                xw_half = held([P, HALF], F32, "h_bf3")
            else:
                xw_half = ring.tile([P, HALF], F32, name="xw_half", align_bytes=64)
            multiply(xw_half[:], copy_x(i, lo, hi, x_bank)[:], wgo_sb[:, lo:hi])
            multiply(y_tiles[i][:, lo:hi], xw_half[:], copy_c(i, lo, hi, c_bank)[:])
            scatter(i, lo, hi, y_tiles[i])
            if c == 1:
                store(i)
